import numpy as np
import ml_dtypes


def mxq(x, axis, fmt="e4m3"):
    dtype, down = {"e4m3": (ml_dtypes.float8_e4m3fn, 7), "e5m2": (ml_dtypes.float8_e5m2, 14)}[fmt]
    v = np.moveaxis(np.asarray(x, np.float32).astype(ml_dtypes.bfloat16).astype(np.float64), axis, -1)
    blocks = v.reshape(v.shape[:-1] + (-1, 32))
    amax = np.abs(blocks).max(-1, keepdims=True)
    byte = np.maximum(np.where(amax > 0, np.frexp(amax)[1] - 1 + 127, 0) - down, 1)
    scale = np.exp2(byte - 127.0)
    codes = (blocks / scale).astype(np.float32).astype(dtype).astype(np.float64)
    return np.moveaxis((codes * scale).reshape(v.shape), -1, axis)


WIDE = False


def mx_kscale(k):
    if not WIDE:
        return np.ones(k)
    levels = np.array([10, -10, 5, -5, 0])
    if k % 512:
        return np.exp2(np.random.permutation(np.resize(levels, k // 32))).repeat(32)
    a = np.empty((k // 512, 16))
    for p in range(k // 512):
        a[p, :8] = np.random.permutation(np.resize(levels, 8))
        for g in range(8):
            far = levels[np.abs(levels - a[p, g]) >= 10]
            a[p, g + 8] = far[np.random.randint(len(far))]
    return np.exp2(a.ravel()).repeat(32)


def f64(x):
    return np.asarray(x).astype(np.float64)


def striped(idx):
    return np.tile(idx.reshape(-1, 16).T, (8, 1)).astype(np.uint16)


def unstriped(offs):
    return offs[:16].T.reshape(-1).astype(np.int64)


E2M1 = np.array([0.0, 0.5, 1.0, 1.5, 2.0, 3.0, 4.0, 6.0, -0.0, -0.5, -1.0, -1.5, -2.0, -3.0, -4.0, -6.0])


def pack_weight(w, fmt):
    k, n = w.shape
    w = f64(np.asarray(w, np.float32).astype(ml_dtypes.bfloat16)).reshape(k // 32, 32, n)
    amax = np.abs(w).max(1)
    if fmt == "e4m3":
        byte = np.frexp(amax)[1] - 1 + 127 - 7
    else:
        mant, ex = np.frexp(amax / 6.0)
        byte = np.where(mant > 0.5, ex, ex - 1) + 127
    byte = np.clip(np.where(amax > 0, byte, 1), 1, 254)
    scaled = (w * np.exp2(127.0 - byte)[:, None, :]).reshape(k, n).astype(np.float32)
    by_word = np.ascontiguousarray(scaled.reshape(k // 512, 128, 4, n).transpose(0, 1, 3, 2))
    if fmt == "e4m3":
        words = by_word.astype(ml_dtypes.float8_e4m3fn).view(np.uint8)
    else:
        c = by_word.astype(ml_dtypes.float4_e2m1fn).view(np.uint8) & 0xF
        words = (c[..., 0::2] | (c[..., 1::2] << 4)).reshape(k // 512, 128, 2 * n)
    return np.ascontiguousarray(words), np.ascontiguousarray(byte.astype(np.uint8).reshape(k // 512, 16, n))


def unpack_weight(words, scales, fmt):
    g, _, n = scales.shape
    words = np.ascontiguousarray(words).reshape(g, 128, n, -1)
    if fmt == "e4m3":
        vals = words.view(ml_dtypes.float8_e4m3fn).astype(np.float64)
    else:
        nib = np.empty((g, 128, n, 4), np.uint8)
        nib[..., 0::2] = words & 0xF
        nib[..., 1::2] = words >> 4
        vals = E2M1[nib]
    vals = vals * np.repeat(np.exp2(scales.astype(np.float64) - 127.0), 8, axis=1)[..., None]
    return vals.transpose(0, 1, 3, 2).reshape(g * 512, n)


def silu(v):
    return v / (1.0 + np.exp(-np.maximum(v, -700.0)))


K, M, T, S = 1536, 1024, 4096, 2048


def setup_inputs():
    n = np.random.standard_normal
    s = mx_kscale(K)[:, None]
    w = n((K, M)) / np.sqrt(K) / s
    v = pack_weight(n((K, T)) * s, "e4m3")
    p_w4 = pack_weight(w[512:], "e2m1")
    return {
        "tab_words": v[0],
        "tab_scales": v[1],
        "w8": (w[:512]).astype(np.float32),
        "w4_words": p_w4[0],
        "w4_scales": p_w4[1],
        "gT": n((M, T)).astype(np.float32),
        "b": (0.3 * n(1024)).astype(np.float32),
        "offs": striped(np.random.permutation(T)[:S]),
    }


def reference(tab_words, tab_scales, w8, w4_words, w4_scales, gT, b, offs):
    tab_ = unpack_weight(tab_words, tab_scales, "e4m3")[:, unstriped(offs)]
    w8_ = mxq(f64(w8), 0, "e4m3")
    w4_ = unpack_weight(w4_words, w4_scales, "e2m1")
    y = w8_.T @ tab_[:512] + w4_.T @ tab_[512:]
    return (silu(y + f64(b)[:, None])) * f64(gT)[:, unstriped(offs)]

@@ -1,0 +1,153 @@
+from contextlib import ExitStack
+
+import concourse.mybir as mybir
+from concourse.masks import make_identity
+
+K, M, T, S = 1536, 1024, 4096, 2048
+FLOPS = 2 * K * M * S
+
+F32 = mybir.dt.float32
+BF16 = mybir.dt.bfloat16
+I32 = mybir.dt.int32
+U32 = mybir.dt.uint32
+U16 = mybir.dt.uint16
+U8 = mybir.dt.uint8
+FP8X4 = mybir.dt.float8_e4m3fn_x4
+FP4X4 = mybir.dt.float4_e2m1fn_x4
+SILU = mybir.ActivationFunctionType.Silu
+MULT = mybir.AluOpType.mult
+
+P = 128
+PACK = 4
+BANK = 512
+STRIPE = 16
+ROW_TILES = M // P
+SLICES = S // BANK
+QUADS = 4
+W8_SHIFT = 4
+
+
+def tile_list_tabgate_silu_kernel(
+    tc, tab_words, tab_scales, w8, w4_words, w4_scales, gT, b, offs, out
+):
+    nc = tc.nc
+    with ExitStack() as ctx:
+        keep = ctx.enter_context(tc.tile_pool(name="keep", bufs=1))
+        wide = ctx.enter_context(tc.tile_pool(name="wide", bufs=9))
+        acts = ctx.enter_context(tc.tile_pool(name="acts", bufs=3))
+        psum = ctx.enter_context(tc.psum_pool(name="psum", bufs=8))
+
+        offsets = keep.tile([P, S // STRIPE], U16, name="offsets")
+        nc.sync.dma_start(offsets[:], offs)
+
+        def listed(s):
+            return offsets[:, s * BANK // STRIPE : (s + 1) * BANK // STRIPE]
+
+        ident = keep.tile([P, P], F32, name="ident")
+        make_identity(nc, ident[:])
+        b_rows = keep.tile([P, P], F32, name="b_rows")
+        nc.gpsimd.memset(b_rows[:], 0.0)
+        nc.gpsimd.dma_start(out=b_rows[0:ROW_TILES, :], in_=b.rearrange("(i p) -> i p", p=P))
+        b_turned = psum.tile([P, BANK], F32, name="acc", tag="acc")
+        nc.tensor.transpose(b_turned[:, 0:P], b_rows[:], ident[:])
+        bias = keep.tile([P, ROW_TILES], F32, name="bias")
+        nc.scalar.copy(out=bias[:], in_=b_turned[:, 0:ROW_TILES])
+
+        scale_rows = keep.tile([P, 2, T // 4], I32, name="scale_rows", align_bytes=64)
+        nc.vector.memset(scale_rows[:], 0)
+        w4_planes = keep.tile([P, 2, M // 4], I32, name="w4_planes", align_bytes=64)
+        nc.vector.memset(w4_planes[:], 0)
+        tab_scales_i = tab_scales.bitcast(I32)
+        for q in range(QUADS):
+            nc.gpsimd.dma_start(
+                out=scale_rows[32 * q : 32 * q + 4, :, :],
+                in_=tab_scales_i[1:3, 4 * q : 4 * q + 4, :].rearrange("a r t -> r a t"),
+            )
+        for q in range(QUADS):
+            nc.gpsimd.dma_start(
+                out=scale_rows[32 * q + W8_SHIFT : 32 * q + W8_SHIFT + 4, 0, :],
+                in_=tab_scales_i[0, 4 * q : 4 * q + 4, :],
+            )
+
+        table = []
+        for a in range(3):
+            words = wide.tile([P, T], I32, name="wide_tile", tag="wide")
+            nc.sync.dma_start(out=words[:], in_=tab_words[a].rearrange("p t i -> p (t i)").bitcast(I32))
+            table.append(words)
+        w8_raw = wide.tile([P, PACK, M], F32, name="wide_tile", tag="wide")
+        nc.sync.dma_start(out=w8_raw[:], in_=w8.rearrange("(p j) n -> p j n", j=PACK))
+        w4_codes = keep.tile([P, 2, 2 * M // 4], I32, name="w4_codes", align_bytes=64)
+        nc.sync.dma_start(out=w4_codes[:], in_=w4_words.bitcast(I32).rearrange("a p n -> p a n"))
+        w4_scales_i = w4_scales.bitcast(I32)
+        for q in range(QUADS):
+            nc.gpsimd.dma_start(
+                out=w4_planes[32 * q : 32 * q + 4, :, :],
+                in_=w4_scales_i[:, 4 * q : 4 * q + 4, :].rearrange("a r n -> r a n"),
+            )
+
+        picked = [keep.tile([P, S], U32, name=f"picked{a}", align_bytes=64) for a in range(3)]
+        planes = [keep.tile([P, S], U8, name=f"planes{c}", align_bytes=64) for c in range(2)]
+        for a in range(2):
+            nc.vector.tensor_copy(picked[a][:], table[a][:].bitcast(U32).indirect(offsets[:]))
+        for c in range(2):
+            nc.vector.tensor_copy(planes[c][:], scale_rows[:, c, :].bitcast(U8).indirect(offsets[:]))
+
+        w8_grouped = keep.tile([P, M, PACK], BF16, name="w8_grouped", align_bytes=64)
+        w8_codes = keep.tile([P, M], U32, name="w8_codes", align_bytes=64)
+        w8_plane = keep.tile([P, M], U8, name="w8_plane", align_bytes=64)
+        for h in range(2):
+            cols = slice(h * M // 2, (h + 1) * M // 2)
+            nc.scalar.copy(out=w8_grouped[:, cols, :], in_=w8_raw[:, :, cols].rearrange("p j n -> p n j"))
+            nc.vector.quantize_mx(
+                out=w8_codes[:, cols].bitcast(FP8X4),
+                scales=w8_plane[:, cols],
+                in_=w8_grouped[:, cols, :].rearrange("p n j -> p (n j)"),
+            )
+        for s in range(SLICES):
+            nc.vector.tensor_copy(
+                picked[2][:, s * BANK : (s + 1) * BANK], table[2][:].bitcast(U32).indirect(listed(s))
+            )
+
+        gate_tiles = []
+        for i in range(ROW_TILES):
+            gate_tile = wide.tile([P, T], F32, name="wide_tile", tag="wide")
+            nc.sync.dma_start(out=gate_tile[:], in_=gT[i * P : (i + 1) * P, :])
+            gate_tiles.append(gate_tile)
+
+        for i in range(ROW_TILES):
+            rows = slice(i * P, (i + 1) * P)
+            gates = gate_tiles[i]
+            act = acts.tile([P, S], F32, name="act")
+            for s in range(SLICES):
+                cols = slice(s * BANK, (s + 1) * BANK)
+                acc = psum.tile([P, BANK], F32, name="acc", tag="acc")
+                nc.tensor.matmul_mx(
+                    out=acc[:],
+                    lhsT=w8_codes[:, rows].bitcast(FP8X4),
+                    lhsT_scale=w8_plane[:, rows],
+                    rhs=picked[0][:, cols].bitcast(FP8X4),
+                    rhs_scale=planes[0][W8_SHIFT:P, cols],
+                    start=True,
+                    stop=False,
+                )
+                for c in range(2):
+                    nc.tensor.matmul_mx(
+                        out=acc[:],
+                        lhsT=w4_codes[:, c, :].bitcast(U8)[:, 2 * i * P : 2 * (i + 1) * P].bitcast(FP4X4),
+                        lhsT_scale=w4_planes[:, c, :].bitcast(U8)[:, rows],
+                        rhs=picked[1 + c][:, cols].bitcast(FP8X4),
+                        rhs_scale=planes[c][:, cols],
+                        start=False,
+                        stop=(c == 1),
+                    )
+                nc.scalar.activation(out=act[:, cols], in_=acc[:], func=SILU, bias=bias[:, i : i + 1])
+            if i % 2 == 0:
+                result_pair = wide.tile([P, 2, S], F32, name="wide_tile", tag="wide")
+            result = result_pair[:, i % 2, :]
+            if i == 0:
+                for s in range(SLICES):
+                    cols = slice(s * BANK, (s + 1) * BANK)
+                    nc.vector.tensor_tensor(result[:, cols], gates[:].indirect(listed(s)), act[:, cols], MULT)
+            else:
+                nc.vector.tensor_tensor(result, gates[:].indirect(offsets[:]), act[:], MULT)
+            nc.sync.dma_start(out=out[rows, :], in_=result)

@@ -24,7 +24,11 @@ STRIPE = 16
 ROW_TILES = M // P
 SLICES = S // BANK
 QUADS = 4
-W8_SHIFT = 4
+W8_SHIFT = 12
+WINDOW_RUNS = (
+    ((0, 12, 16), (12, 44, 0), (44, 76, 4), (76, 108, 8), (108, 128, 12)),
+    ((0, 4, 32), (4, 36, 8), (36, 68, 12), (68, 100, 16), (100, 128, 0)),
+)
 
 
 def tile_list_tabgate_silu_kernel(
@@ -43,54 +47,53 @@ def tile_list_tabgate_silu_kernel(
         def listed(s):
             return offsets[:, s * BANK // STRIPE : (s + 1) * BANK // STRIPE]
 
-        ident = keep.tile([P, P], F32, name="ident")
-        make_identity(nc, ident[:])
+        w4_planes = keep.tile([P, 2, M // 4], I32, name="w4_planes", align_bytes=64)
+        nc.vector.memset(w4_planes[:], 0)
         b_rows = keep.tile([P, P], F32, name="b_rows")
         nc.gpsimd.memset(b_rows[:], 0.0)
         nc.gpsimd.dma_start(out=b_rows[0:ROW_TILES, :], in_=b.rearrange("(i p) -> i p", p=P))
-        b_turned = psum.tile([P, BANK], F32, name="acc", tag="acc")
-        nc.tensor.transpose(b_turned[:, 0:P], b_rows[:], ident[:])
-        bias = keep.tile([P, ROW_TILES], F32, name="bias")
-        nc.scalar.copy(out=bias[:], in_=b_turned[:, 0:ROW_TILES])
-
-        scale_rows = keep.tile([P, 2, T // 4], I32, name="scale_rows", align_bytes=64)
-        nc.vector.memset(scale_rows[:], 0)
-        w4_planes = keep.tile([P, 2, M // 4], I32, name="w4_planes", align_bytes=64)
-        nc.vector.memset(w4_planes[:], 0)
-        tab_scales_i = tab_scales.bitcast(I32)
-        for q in range(QUADS):
-            nc.gpsimd.dma_start(
-                out=scale_rows[32 * q : 32 * q + 4, :, :],
-                in_=tab_scales_i[1:3, 4 * q : 4 * q + 4, :].rearrange("a r t -> r a t"),
-            )
-        for q in range(QUADS):
-            nc.gpsimd.dma_start(
-                out=scale_rows[32 * q + W8_SHIFT : 32 * q + W8_SHIFT + 4, 0, :],
-                in_=tab_scales_i[0, 4 * q : 4 * q + 4, :],
-            )
-
-        table = []
-        for a in range(3):
-            words = wide.tile([P, T], I32, name="wide_tile", tag="wide")
-            nc.sync.dma_start(out=words[:], in_=tab_words[a].rearrange("p t i -> p (t i)").bitcast(I32))
-            table.append(words)
-        w8_raw = wide.tile([P, PACK, M], F32, name="wide_tile", tag="wide")
-        nc.sync.dma_start(out=w8_raw[:], in_=w8.rearrange("(p j) n -> p j n", j=PACK))
-        w4_codes = keep.tile([P, 2, 2 * M // 4], I32, name="w4_codes", align_bytes=64)
-        nc.sync.dma_start(out=w4_codes[:], in_=w4_words.bitcast(I32).rearrange("a p n -> p a n"))
         w4_scales_i = w4_scales.bitcast(I32)
         for q in range(QUADS):
             nc.gpsimd.dma_start(
                 out=w4_planes[32 * q : 32 * q + 4, :, :],
                 in_=w4_scales_i[:, 4 * q : 4 * q + 4, :].rearrange("a r n -> r a n"),
             )
+        ident = keep.tile([P, P], F32, name="ident")
+        make_identity(nc, ident[:])
+        b_turned = psum.tile([P, BANK], F32, name="acc", tag="acc")
+        nc.tensor.transpose(b_turned[:, 0:P], b_rows[:], ident[:])
+        bias = keep.tile([P, ROW_TILES], F32, name="bias")
+        nc.scalar.copy(out=bias[:], in_=b_turned[:, 0:ROW_TILES])
+
+        all_scale_rows = tab_scales.bitcast(I32).rearrange("a q t -> (a q) t")
+        windows = [keep.tile([P, T // 4], I32, name=f"scale_window{c}", align_bytes=64) for c in range(2)]
+        table = [wide.tile([P, T], I32, name="wide_tile", tag="wide") for a in range(3)]
+
+        def load_words(a):
+            nc.sync.dma_start(out=table[a][:], in_=tab_words[a].rearrange("p t i -> p (t i)").bitcast(I32))
+
+        def load_scale_window(c):
+            for first, last, row in WINDOW_RUNS[c]:
+                count = last - first
+                queue = nc.scalar if (c, last) == (1, P) else nc.sync
+                queue.dma_start(out=windows[c][first:last, :], in_=all_scale_rows[row : row + count, :])
+
+        load_scale_window(1)
+        load_words(0)
+        load_words(1)
+        load_scale_window(0)
+        w8_raw = wide.tile([P, PACK, M], F32, name="wide_tile", tag="wide")
+        nc.sync.dma_start(out=w8_raw[:], in_=w8.rearrange("(p j) n -> p j n", j=PACK))
+        load_words(2)
+        w4_codes = keep.tile([P, 2, 2 * M // 4], I32, name="w4_codes", align_bytes=64)
+        nc.sync.dma_start(out=w4_codes[:], in_=w4_words.bitcast(I32).rearrange("a p n -> p a n"))
 
         picked = [keep.tile([P, S], U32, name=f"picked{a}", align_bytes=64) for a in range(3)]
         planes = [keep.tile([P, S], U8, name=f"planes{c}", align_bytes=64) for c in range(2)]
+        nc.vector.tensor_copy(planes[1][:], windows[1][:].bitcast(U8).indirect(offsets[:]))
         for a in range(2):
             nc.vector.tensor_copy(picked[a][:], table[a][:].bitcast(U32).indirect(offsets[:]))
-        for c in range(2):
-            nc.vector.tensor_copy(planes[c][:], scale_rows[:, c, :].bitcast(U8).indirect(offsets[:]))
+        nc.vector.tensor_copy(planes[0][:], windows[0][:].bitcast(U8).indirect(offsets[:]))
 
         w8_grouped = keep.tile([P, M, PACK], BF16, name="w8_grouped", align_bytes=64)
         w8_codes = keep.tile([P, M], U32, name="w8_codes", align_bytes=64)
@@ -148,6 +151,13 @@ def tile_list_tabgate_silu_kernel(
                 for s in range(SLICES):
                     cols = slice(s * BANK, (s + 1) * BANK)
                     nc.vector.tensor_tensor(result[:, cols], gates[:].indirect(listed(s)), act[:, cols], MULT)
-            else:
+            elif i < ROW_TILES - 1:
                 nc.vector.tensor_tensor(result, gates[:].indirect(offsets[:]), act[:], MULT)
-            nc.sync.dma_start(out=out[rows, :], in_=result)
+            if i < ROW_TILES - 1:
+                nc.sync.dma_start(out=out[rows, :], in_=result)
+            else:
+                for h in range(2):
+                    cols = slice(h * S // 2, (h + 1) * S // 2)
+                    half = offsets[:, h * S // (2 * STRIPE) : (h + 1) * S // (2 * STRIPE)]
+                    nc.vector.tensor_tensor(result[:, cols], gates[:].indirect(half), act[:, cols], MULT)
+                    nc.sync.dma_start(out=out[rows, cols], in_=result[:, cols])

@@ -48,7 +48,7 @@ def tile_list_tabgate_silu_kernel(
             return offsets[:, s * BANK // STRIPE : (s + 1) * BANK // STRIPE]
 
         w4_planes = keep.tile([P, 2, M // 4], I32, name="w4_planes", align_bytes=64)
-        nc.vector.memset(w4_planes[:], 0)
+        nc.gpsimd.memset(w4_planes[:], 0)
         b_rows = keep.tile([P, P], F32, name="b_rows")
         nc.gpsimd.memset(b_rows[:], 0.0)
         nc.gpsimd.dma_start(out=b_rows[0:ROW_TILES, :], in_=b.rearrange("(i p) -> i p", p=P))
@@ -75,8 +75,7 @@ def tile_list_tabgate_silu_kernel(
         def load_scale_window(c):
             for first, last, row in WINDOW_RUNS[c]:
                 count = last - first
-                queue = nc.scalar if (c, last) == (1, P) else nc.sync
-                queue.dma_start(out=windows[c][first:last, :], in_=all_scale_rows[row : row + count, :])
+                nc.sync.dma_start(out=windows[c][first:last, :], in_=all_scale_rows[row : row + count, :])
 
         load_scale_window(1)
         load_words(0)
@@ -153,7 +152,11 @@ def tile_list_tabgate_silu_kernel(
                     nc.vector.tensor_tensor(result[:, cols], gates[:].indirect(listed(s)), act[:, cols], MULT)
             elif i < ROW_TILES - 1:
                 nc.vector.tensor_tensor(result, gates[:].indirect(offsets[:]), act[:], MULT)
-            if i < ROW_TILES - 1:
+            if i < ROW_TILES - 2:
+                if i % 2 == 1:
+                    pair_rows = out[(i - 1) * P : (i + 1) * P, :].rearrange("(h p) j -> p h j", p=P)
+                    nc.sync.dma_start(out=pair_rows, in_=result_pair[:])
+            elif i < ROW_TILES - 1:
                 nc.sync.dma_start(out=out[rows, :], in_=result)
             else:
                 for h in range(2):

@@ -25,10 +25,8 @@ ROW_TILES = M // P
 SLICES = S // BANK
 QUADS = 4
 W8_SHIFT = 12
-WINDOW_RUNS = (
-    ((0, 12, 16), (12, 44, 0), (44, 76, 4), (76, 108, 8), (108, 128, 12)),
-    ((0, 4, 32), (4, 36, 8), (36, 68, 12), (68, 100, 16), (100, 128, 0)),
-)
+WINDOW_RUNS = ((12, 44, 0), (76, 108, 8), (44, 76, 4), (0, 4, 16), (4, 12, 40), (108, 128, 12))
+LAST_PASS_AT = (100, 104, 4, 8)
 
 
 def tile_list_tabgate_silu_kernel(
@@ -66,33 +64,33 @@ def tile_list_tabgate_silu_kernel(
         nc.scalar.copy(out=bias[:], in_=b_turned[:, 0:ROW_TILES])
 
         all_scale_rows = tab_scales.bitcast(I32).rearrange("a q t -> (a q) t")
-        windows = [keep.tile([P, T // 4], I32, name=f"scale_window{c}", align_bytes=64) for c in range(2)]
-        table = [wide.tile([P, T], I32, name="wide_tile", tag="wide") for a in range(3)]
+        window = keep.tile([P, T // 4], I32, name="scale_window", align_bytes=256)
+        table = [wide.tile([P, T], I32, name="wide_tile", tag="wide", align_bytes=256) for a in range(3)]
 
         def load_words(a):
             nc.sync.dma_start(out=table[a][:], in_=tab_words[a].rearrange("p t i -> p (t i)").bitcast(I32))
 
-        def load_scale_window(c):
-            for first, last, row in WINDOW_RUNS[c]:
-                count = last - first
-                nc.sync.dma_start(out=windows[c][first:last, :], in_=all_scale_rows[row : row + count, :])
-
-        load_scale_window(1)
+        for first, last, row in WINDOW_RUNS:
+            nc.sync.dma_start(out=window[first:last, :], in_=all_scale_rows[row : row + last - first, :])
         load_words(0)
         load_words(1)
-        load_scale_window(0)
-        w8_raw = wide.tile([P, PACK, M], F32, name="wide_tile", tag="wide")
+        w8_raw = wide.tile([P, PACK, M], F32, name="wide_tile", tag="wide", align_bytes=256)
         nc.sync.dma_start(out=w8_raw[:], in_=w8.rearrange("(p j) n -> p j n", j=PACK))
         load_words(2)
-        w4_codes = keep.tile([P, 2, 2 * M // 4], I32, name="w4_codes", align_bytes=64)
+        w4_codes = keep.tile([P, 2, 2 * M // 4], I32, name="w4_codes", align_bytes=256)
         nc.sync.dma_start(out=w4_codes[:], in_=w4_words.bitcast(I32).rearrange("a p n -> p a n"))
 
         picked = [keep.tile([P, S], U32, name=f"picked{a}", align_bytes=64) for a in range(3)]
         planes = [keep.tile([P, S], U8, name=f"planes{c}", align_bytes=64) for c in range(2)]
-        nc.vector.tensor_copy(planes[1][:], windows[1][:].bitcast(U8).indirect(offsets[:]))
+        nc.gpsimd.memset(planes[1][:].bitcast(I32), 0)
+        nc.vector.tensor_copy(planes[0][:], window[:].bitcast(U8).indirect(offsets[:]))
+        for q in range(QUADS):
+            nc.gpsimd.dma_start(
+                out=planes[1][32 * q : 32 * q + 4, :].bitcast(I32),
+                in_=planes[0][LAST_PASS_AT[q] : LAST_PASS_AT[q] + 4, :].bitcast(I32),
+            )
         for a in range(2):
             nc.vector.tensor_copy(picked[a][:], table[a][:].bitcast(U32).indirect(offsets[:]))
-        nc.vector.tensor_copy(planes[0][:], windows[0][:].bitcast(U8).indirect(offsets[:]))
 
         w8_grouped = keep.tile([P, M, PACK], BF16, name="w8_grouped", align_bytes=64)
         w8_codes = keep.tile([P, M], U32, name="w8_codes", align_bytes=64)
@@ -112,7 +110,7 @@ def tile_list_tabgate_silu_kernel(
 
         gate_tiles = []
         for i in range(ROW_TILES):
-            gate_tile = wide.tile([P, T], F32, name="wide_tile", tag="wide")
+            gate_tile = wide.tile([P, T], F32, name="wide_tile", tag="wide", align_bytes=256)
             nc.sync.dma_start(out=gate_tile[:], in_=gT[i * P : (i + 1) * P, :])
             gate_tiles.append(gate_tile)
 
@@ -144,7 +142,7 @@ def tile_list_tabgate_silu_kernel(
                     )
                 nc.scalar.activation(out=act[:, cols], in_=acc[:], func=SILU, bias=bias[:, i : i + 1])
             if i % 2 == 0:
-                result_pair = wide.tile([P, 2, S], F32, name="wide_tile", tag="wide")
+                result_pair = wide.tile([P, 2, S], F32, name="wide_tile", tag="wide", align_bytes=256)
             result = result_pair[:, i % 2, :]
             if i == 0:
                 for s in range(SLICES):

@@ -19,42 +19,60 @@ MULT = mybir.AluOpType.mult
 
 P = 128
 PACK = 4
+PASSES = K // (P * PACK)
+W4_PASSES = PASSES - 1
+W4_WORD_BYTES = 2
+BYTES_PER_I32 = 4
 BANK = 512
 STRIPE = 16
 ROW_TILES = M // P
-SLICES = S // BANK
 QUADS = 4
-W8_SHIFT = 12
+QUAD = P // QUADS
+QUAD_BLOCKS = 4
+MX_ALIGN = 64
+DMA_ALIGN = 256
+
+PASS0_SHIFT = 12
 WINDOW_RUNS = ((12, 44, 0), (76, 108, 8), (44, 76, 4), (0, 4, 16), (4, 12, 40), (108, 128, 12))
-LAST_PASS_AT = (100, 104, 4, 8)
+PASS2_AT = (100, 104, 4, 8)
+
+WIDE_SLOTS = 9
+ACT_SLOTS = 3
+PSUM_BANKS = 8
+W8_CHUNKS = 2
+LAST_TILE_PIECES = ((0, S // 2), (S // 2, 3 * S // 4), (3 * S // 4, S))
 
 
 def tile_list_tabgate_silu_kernel(
     tc, tab_words, tab_scales, w8, w4_words, w4_scales, gT, b, offs, out
 ):
     nc = tc.nc
+    token_slices = [slice(j, j + BANK) for j in range(0, S, BANK)]
     with ExitStack() as ctx:
         keep = ctx.enter_context(tc.tile_pool(name="keep", bufs=1))
-        wide = ctx.enter_context(tc.tile_pool(name="wide", bufs=9))
-        acts = ctx.enter_context(tc.tile_pool(name="acts", bufs=3))
-        psum = ctx.enter_context(tc.psum_pool(name="psum", bufs=8))
+        wide = ctx.enter_context(tc.tile_pool(name="wide", bufs=WIDE_SLOTS))
+        acts = ctx.enter_context(tc.tile_pool(name="acts", bufs=ACT_SLOTS))
+        psum = ctx.enter_context(tc.psum_pool(name="psum", bufs=PSUM_BANKS))
+
+        def wide_tile(shape, dtype):
+            return wide.tile(shape, dtype, name="wide_tile", tag="wide", align_bytes=DMA_ALIGN)
 
         offsets = keep.tile([P, S // STRIPE], U16, name="offsets")
         nc.sync.dma_start(offsets[:], offs)
 
-        def listed(s):
-            return offsets[:, s * BANK // STRIPE : (s + 1) * BANK // STRIPE]
+        def entries(cols):
+            return offsets[:, cols.start // STRIPE : cols.stop // STRIPE]
 
-        w4_planes = keep.tile([P, 2, M // 4], I32, name="w4_planes", align_bytes=64)
+        w4_planes = keep.tile([P, W4_PASSES, M // BYTES_PER_I32], I32, name="w4_planes", align_bytes=MX_ALIGN)
         nc.gpsimd.memset(w4_planes[:], 0)
         b_rows = keep.tile([P, P], F32, name="b_rows")
         nc.gpsimd.memset(b_rows[:], 0.0)
         nc.gpsimd.dma_start(out=b_rows[0:ROW_TILES, :], in_=b.rearrange("(i p) -> i p", p=P))
-        w4_scales_i = w4_scales.bitcast(I32)
-        for q in range(QUADS):
+        w4_scale_rows = w4_scales.bitcast(I32)
+        for quad in range(QUADS):
             nc.gpsimd.dma_start(
-                out=w4_planes[32 * q : 32 * q + 4, :, :],
-                in_=w4_scales_i[:, 4 * q : 4 * q + 4, :].rearrange("a r n -> r a n"),
+                out=w4_planes[QUAD * quad : QUAD * quad + QUAD_BLOCKS, :, :],
+                in_=w4_scale_rows[:, QUAD_BLOCKS * quad : QUAD_BLOCKS * (quad + 1), :].rearrange("a r n -> r a n"),
             )
         ident = keep.tile([P, P], F32, name="ident")
         make_identity(nc, ident[:])
@@ -63,54 +81,57 @@ def tile_list_tabgate_silu_kernel(
         bias = keep.tile([P, ROW_TILES], F32, name="bias")
         nc.scalar.copy(out=bias[:], in_=b_turned[:, 0:ROW_TILES])
 
-        all_scale_rows = tab_scales.bitcast(I32).rearrange("a q t -> (a q) t")
-        window = keep.tile([P, T // 4], I32, name="scale_window", align_bytes=256)
-        table = [wide.tile([P, T], I32, name="wide_tile", tag="wide", align_bytes=256) for a in range(3)]
+        table_scale_rows = tab_scales.bitcast(I32).rearrange("a q t -> (a q) t")
+        scale_window = keep.tile([P, T // BYTES_PER_I32], I32, name="scale_window", align_bytes=DMA_ALIGN)
+        table = [wide_tile([P, T], I32) for a in range(PASSES)]
 
         def load_words(a):
             nc.sync.dma_start(out=table[a][:], in_=tab_words[a].rearrange("p t i -> p (t i)").bitcast(I32))
 
         for first, last, row in WINDOW_RUNS:
-            nc.sync.dma_start(out=window[first:last, :], in_=all_scale_rows[row : row + last - first, :])
+            nc.sync.dma_start(out=scale_window[first:last, :], in_=table_scale_rows[row : row + last - first, :])
         load_words(0)
         load_words(1)
-        w8_raw = wide.tile([P, PACK, M], F32, name="wide_tile", tag="wide", align_bytes=256)
-        nc.sync.dma_start(out=w8_raw[:], in_=w8.rearrange("(p j) n -> p j n", j=PACK))
+        w8_raw = wide_tile([P, PACK, M], F32)
+        nc.sync.dma_start(out=w8_raw[:], in_=w8.rearrange("(p t) n -> p t n", t=PACK))
         load_words(2)
-        w4_codes = keep.tile([P, 2, 2 * M // 4], I32, name="w4_codes", align_bytes=256)
+        w4_codes = keep.tile(
+            [P, W4_PASSES, W4_WORD_BYTES * M // BYTES_PER_I32], I32, name="w4_codes", align_bytes=DMA_ALIGN
+        )
         nc.sync.dma_start(out=w4_codes[:], in_=w4_words.bitcast(I32).rearrange("a p n -> p a n"))
 
-        picked = [keep.tile([P, S], U32, name=f"picked{a}", align_bytes=64) for a in range(3)]
-        planes = [keep.tile([P, S], U8, name=f"planes{c}", align_bytes=64) for c in range(2)]
-        nc.gpsimd.memset(planes[1][:].bitcast(I32), 0)
-        nc.vector.tensor_copy(planes[0][:], window[:].bitcast(U8).indirect(offsets[:]))
-        for q in range(QUADS):
+        picked_words = [keep.tile([P, S], U32, name=f"picked{a}", align_bytes=MX_ALIGN) for a in range(PASSES)]
+        picked_scales = keep.tile([P, S], U8, name="planes0", align_bytes=MX_ALIGN)
+        pass2_plane = keep.tile([P, S], U8, name="planes1", align_bytes=MX_ALIGN)
+        nc.gpsimd.memset(pass2_plane[:].bitcast(I32), 0)
+        nc.vector.tensor_copy(picked_scales[:], scale_window[:].bitcast(U8).indirect(offsets[:]))
+        for quad in range(QUADS):
             nc.gpsimd.dma_start(
-                out=planes[1][32 * q : 32 * q + 4, :].bitcast(I32),
-                in_=planes[0][LAST_PASS_AT[q] : LAST_PASS_AT[q] + 4, :].bitcast(I32),
+                out=pass2_plane[QUAD * quad : QUAD * quad + QUAD_BLOCKS, :].bitcast(I32),
+                in_=picked_scales[PASS2_AT[quad] : PASS2_AT[quad] + QUAD_BLOCKS, :].bitcast(I32),
             )
-        for a in range(2):
-            nc.vector.tensor_copy(picked[a][:], table[a][:].bitcast(U32).indirect(offsets[:]))
+        w4_pass_planes = (picked_scales, pass2_plane)
+        for a in range(PASSES - 1):
+            nc.vector.tensor_copy(picked_words[a][:], table[a][:].bitcast(U32).indirect(offsets[:]))
 
-        w8_grouped = keep.tile([P, M, PACK], BF16, name="w8_grouped", align_bytes=64)
-        w8_codes = keep.tile([P, M], U32, name="w8_codes", align_bytes=64)
-        w8_plane = keep.tile([P, M], U8, name="w8_plane", align_bytes=64)
-        for h in range(2):
-            cols = slice(h * M // 2, (h + 1) * M // 2)
-            nc.scalar.copy(out=w8_grouped[:, cols, :], in_=w8_raw[:, :, cols].rearrange("p j n -> p n j"))
+        w8_grouped = keep.tile([P, M, PACK], BF16, name="w8_grouped", align_bytes=MX_ALIGN)
+        w8_codes = keep.tile([P, M], U32, name="w8_codes", align_bytes=MX_ALIGN)
+        w8_plane = keep.tile([P, M], U8, name="w8_plane", align_bytes=MX_ALIGN)
+        for chunk in range(W8_CHUNKS):
+            features = slice(chunk * M // W8_CHUNKS, (chunk + 1) * M // W8_CHUNKS)
+            nc.scalar.copy(out=w8_grouped[:, features, :], in_=w8_raw[:, :, features].rearrange("p t n -> p n t"))
             nc.vector.quantize_mx(
-                out=w8_codes[:, cols].bitcast(FP8X4),
-                scales=w8_plane[:, cols],
-                in_=w8_grouped[:, cols, :].rearrange("p n j -> p (n j)"),
+                out=w8_codes[:, features].bitcast(FP8X4),
+                scales=w8_plane[:, features],
+                in_=w8_grouped[:, features, :].rearrange("p n t -> p (n t)"),
             )
-        for s in range(SLICES):
-            nc.vector.tensor_copy(
-                picked[2][:, s * BANK : (s + 1) * BANK], table[2][:].bitcast(U32).indirect(listed(s))
-            )
+
+        for cols in token_slices:
+            nc.vector.tensor_copy(picked_words[-1][:, cols], table[-1][:].bitcast(U32).indirect(entries(cols)))
 
         gate_tiles = []
         for i in range(ROW_TILES):
-            gate_tile = wide.tile([P, T], F32, name="wide_tile", tag="wide", align_bytes=256)
+            gate_tile = wide_tile([P, T], F32)
             nc.sync.dma_start(out=gate_tile[:], in_=gT[i * P : (i + 1) * P, :])
             gate_tiles.append(gate_tile)
 
@@ -118,47 +139,46 @@ def tile_list_tabgate_silu_kernel(
             rows = slice(i * P, (i + 1) * P)
             gates = gate_tiles[i]
             act = acts.tile([P, S], F32, name="act")
-            for s in range(SLICES):
-                cols = slice(s * BANK, (s + 1) * BANK)
+            for cols in token_slices:
                 acc = psum.tile([P, BANK], F32, name="acc", tag="acc")
                 nc.tensor.matmul_mx(
                     out=acc[:],
                     lhsT=w8_codes[:, rows].bitcast(FP8X4),
                     lhsT_scale=w8_plane[:, rows],
-                    rhs=picked[0][:, cols].bitcast(FP8X4),
-                    rhs_scale=planes[0][W8_SHIFT:P, cols],
+                    rhs=picked_words[0][:, cols].bitcast(FP8X4),
+                    rhs_scale=picked_scales[PASS0_SHIFT:P, cols],
                     start=True,
                     stop=False,
                 )
-                for c in range(2):
+                for c in range(W4_PASSES):
+                    w4_bytes = slice(W4_WORD_BYTES * rows.start, W4_WORD_BYTES * rows.stop)
                     nc.tensor.matmul_mx(
                         out=acc[:],
-                        lhsT=w4_codes[:, c, :].bitcast(U8)[:, 2 * i * P : 2 * (i + 1) * P].bitcast(FP4X4),
+                        lhsT=w4_codes[:, c, :].bitcast(U8)[:, w4_bytes].bitcast(FP4X4),
                         lhsT_scale=w4_planes[:, c, :].bitcast(U8)[:, rows],
-                        rhs=picked[1 + c][:, cols].bitcast(FP8X4),
-                        rhs_scale=planes[c][:, cols],
+                        rhs=picked_words[1 + c][:, cols].bitcast(FP8X4),
+                        rhs_scale=w4_pass_planes[c][:, cols],
                         start=False,
-                        stop=(c == 1),
+                        stop=(c == W4_PASSES - 1),
                     )
                 nc.scalar.activation(out=act[:, cols], in_=acc[:], func=SILU, bias=bias[:, i : i + 1])
+
             if i % 2 == 0:
-                result_pair = wide.tile([P, 2, S], F32, name="wide_tile", tag="wide", align_bytes=256)
+                result_pair = wide_tile([P, 2, S], F32)
             result = result_pair[:, i % 2, :]
-            if i == 0:
-                for s in range(SLICES):
-                    cols = slice(s * BANK, (s + 1) * BANK)
-                    nc.vector.tensor_tensor(result[:, cols], gates[:].indirect(listed(s)), act[:, cols], MULT)
-            elif i < ROW_TILES - 1:
-                nc.vector.tensor_tensor(result, gates[:].indirect(offsets[:]), act[:], MULT)
-            if i < ROW_TILES - 2:
-                if i % 2 == 1:
-                    pair_rows = out[(i - 1) * P : (i + 1) * P, :].rearrange("(h p) j -> p h j", p=P)
-                    nc.sync.dma_start(out=pair_rows, in_=result_pair[:])
-            elif i < ROW_TILES - 1:
-                nc.sync.dma_start(out=out[rows, :], in_=result)
-            else:
-                for h in range(2):
-                    cols = slice(h * S // 2, (h + 1) * S // 2)
-                    half = offsets[:, h * S // (2 * STRIPE) : (h + 1) * S // (2 * STRIPE)]
-                    nc.vector.tensor_tensor(result[:, cols], gates[:].indirect(half), act[:, cols], MULT)
+            if i == ROW_TILES - 1:
+                for first, last in LAST_TILE_PIECES:
+                    cols = slice(first, last)
+                    nc.vector.tensor_tensor(result[:, cols], gates[:].indirect(entries(cols)), act[:, cols], MULT)
                     nc.sync.dma_start(out=out[rows, cols], in_=result[:, cols])
+                continue
+            if i == 0:
+                for cols in token_slices:
+                    nc.vector.tensor_tensor(result[:, cols], gates[:].indirect(entries(cols)), act[:, cols], MULT)
+            else:
+                nc.vector.tensor_tensor(result, gates[:].indirect(offsets[:]), act[:], MULT)
+            if i == ROW_TILES - 2:
+                nc.sync.dma_start(out=out[rows, :], in_=result)
+            elif i % 2 == 1:
+                pair_rows = out[(i - 1) * P : (i + 1) * P, :].rearrange("(h p) j -> p h j", p=P)
+                nc.sync.dma_start(out=pair_rows, in_=result_pair[:])

@@ -36,7 +36,7 @@ PASS0_SHIFT = 12
 WINDOW_RUNS = ((12, 44, 0), (76, 108, 8), (44, 76, 4), (0, 4, 16), (4, 12, 40), (108, 128, 12))
 PASS2_AT = (100, 104, 4, 8)
 
-WIDE_SLOTS = 9
+WIDE_SLOTS = 6
 ACT_SLOTS = 3
 PSUM_BANKS = 8
 W8_CHUNKS = 2
@@ -51,6 +51,7 @@ def tile_list_tabgate_silu_kernel(
     with ExitStack() as ctx:
         keep = ctx.enter_context(tc.tile_pool(name="keep", bufs=1))
         wide = ctx.enter_context(tc.tile_pool(name="wide", bufs=WIDE_SLOTS))
+        results = ctx.enter_context(tc.tile_pool(name="results", bufs=ROW_TILES // 2))
         acts = ctx.enter_context(tc.tile_pool(name="acts", bufs=ACT_SLOTS))
         psum = ctx.enter_context(tc.psum_pool(name="psum", bufs=PSUM_BANKS))
 
@@ -64,26 +65,18 @@ def tile_list_tabgate_silu_kernel(
             return offsets[:, cols.start // STRIPE : cols.stop // STRIPE]
 
         w4_planes = keep.tile([P, W4_PASSES, M // BYTES_PER_I32], I32, name="w4_planes", align_bytes=MX_ALIGN)
-        nc.gpsimd.memset(w4_planes[:], 0)
+        nc.vector.memset(w4_planes[:], 0)
         b_rows = keep.tile([P, P], F32, name="b_rows")
-        nc.gpsimd.memset(b_rows[:], 0.0)
-        nc.gpsimd.dma_start(out=b_rows[0:ROW_TILES, :], in_=b.rearrange("(i p) -> i p", p=P))
-        w4_scale_rows = w4_scales.bitcast(I32)
-        for quad in range(QUADS):
-            nc.gpsimd.dma_start(
-                out=w4_planes[QUAD * quad : QUAD * quad + QUAD_BLOCKS, :, :],
-                in_=w4_scale_rows[:, QUAD_BLOCKS * quad : QUAD_BLOCKS * (quad + 1), :].rearrange("a r n -> r a n"),
-            )
+        nc.vector.memset(b_rows[:], 0.0)
         ident = keep.tile([P, P], F32, name="ident")
         make_identity(nc, ident[:])
-        b_turned = psum.tile([P, BANK], F32, name="acc", tag="acc")
-        nc.tensor.transpose(b_turned[:, 0:P], b_rows[:], ident[:])
-        bias = keep.tile([P, ROW_TILES], F32, name="bias")
-        nc.scalar.copy(out=bias[:], in_=b_turned[:, 0:ROW_TILES])
 
         table_scale_rows = tab_scales.bitcast(I32).rearrange("a q t -> (a q) t")
-        scale_window = keep.tile([P, T // BYTES_PER_I32], I32, name="scale_window", align_bytes=DMA_ALIGN)
-        table = [wide_tile([P, T], I32) for a in range(PASSES)]
+        scale_window = wide_tile([P, T // BYTES_PER_I32], I32)
+        table = [wide_tile([P, T], I32) for a in range(PASSES - 1)]
+        w8_raw = wide_tile([P, PACK, M], F32)
+        w8_grouped = wide_tile([P, M, PACK], BF16)
+        table.append(wide_tile([P, T], I32))
 
         def load_words(a):
             nc.sync.dma_start(out=table[a][:], in_=tab_words[a].rearrange("p t i -> p (t i)").bitcast(I32))
@@ -91,8 +84,18 @@ def tile_list_tabgate_silu_kernel(
         for first, last, row in WINDOW_RUNS:
             nc.sync.dma_start(out=scale_window[first:last, :], in_=table_scale_rows[row : row + last - first, :])
         load_words(0)
+        w4_scale_rows = w4_scales.bitcast(I32)
+        for quad in range(QUADS):
+            nc.sync.dma_start(
+                out=w4_planes[QUAD * quad : QUAD * quad + QUAD_BLOCKS, :, :],
+                in_=w4_scale_rows[:, QUAD_BLOCKS * quad : QUAD_BLOCKS * (quad + 1), :].rearrange("a r n -> r a n"),
+            )
+        nc.sync.dma_start(out=b_rows[0:ROW_TILES, :], in_=b.rearrange("(i p) -> i p", p=P))
+        b_turned = psum.tile([P, BANK], F32, name="acc", tag="acc")
+        nc.tensor.transpose(b_turned[:, 0:P], b_rows[:], ident[:])
+        bias = keep.tile([P, ROW_TILES], F32, name="bias")
+        nc.scalar.copy(out=bias[:], in_=b_turned[:, 0:ROW_TILES])
         load_words(1)
-        w8_raw = wide_tile([P, PACK, M], F32)
         nc.sync.dma_start(out=w8_raw[:], in_=w8.rearrange("(p t) n -> p t n", t=PACK))
         load_words(2)
         w4_codes = keep.tile(
@@ -106,7 +109,7 @@ def tile_list_tabgate_silu_kernel(
         nc.gpsimd.memset(pass2_plane[:].bitcast(I32), 0)
         nc.vector.tensor_copy(picked_scales[:], scale_window[:].bitcast(U8).indirect(offsets[:]))
         for quad in range(QUADS):
-            nc.gpsimd.dma_start(
+            nc.sync.dma_start(
                 out=pass2_plane[QUAD * quad : QUAD * quad + QUAD_BLOCKS, :].bitcast(I32),
                 in_=picked_scales[PASS2_AT[quad] : PASS2_AT[quad] + QUAD_BLOCKS, :].bitcast(I32),
             )
@@ -114,7 +117,6 @@ def tile_list_tabgate_silu_kernel(
         for a in range(PASSES - 1):
             nc.vector.tensor_copy(picked_words[a][:], table[a][:].bitcast(U32).indirect(offsets[:]))
 
-        w8_grouped = keep.tile([P, M, PACK], BF16, name="w8_grouped", align_bytes=MX_ALIGN)
         w8_codes = keep.tile([P, M], U32, name="w8_codes", align_bytes=MX_ALIGN)
         w8_plane = keep.tile([P, M], U8, name="w8_plane", align_bytes=MX_ALIGN)
         for chunk in range(W8_CHUNKS):
@@ -164,7 +166,7 @@ def tile_list_tabgate_silu_kernel(
                 nc.scalar.activation(out=act[:, cols], in_=acc[:], func=SILU, bias=bias[:, i : i + 1])
 
             if i % 2 == 0:
-                result_pair = wide_tile([P, 2, S], F32)
+                result_pair = results.tile([P, 2, S], F32, name="result_pair", align_bytes=DMA_ALIGN)
             result = result_pair[:, i % 2, :]
             if i == ROW_TILES - 1:
                 for first, last in LAST_TILE_PIECES:

@@ -33,13 +33,13 @@ MX_ALIGN = 64
 DMA_ALIGN = 256
 
 PASS0_SHIFT = 12
-WINDOW_RUNS = ((12, 44, 0), (76, 108, 8), (44, 76, 4), (0, 4, 16), (4, 12, 40), (108, 128, 12))
+WINDOW_RUNS = ((108, 128, 12), (12, 44, 0), (76, 108, 8), (44, 76, 4), (0, 4, 16), (4, 12, 40))
 PASS2_AT = (100, 104, 4, 8)
 
 WIDE_SLOTS = 6
 ACT_SLOTS = 3
 PSUM_BANKS = 8
-W8_CHUNKS = 2
+W8_CHUNK = M // 2
 LAST_TILE_PIECES = ((0, S // 2), (S // 2, 3 * S // 4), (3 * S // 4, S))
 
 
@@ -73,16 +73,18 @@ def tile_list_tabgate_silu_kernel(
 
         table_scale_rows = tab_scales.bitcast(I32).rearrange("a q t -> (a q) t")
         scale_window = wide_tile([P, T // BYTES_PER_I32], I32)
-        table = [wide_tile([P, T], I32) for a in range(PASSES - 1)]
-        w8_raw = wide_tile([P, PACK, M], F32)
-        w8_grouped = wide_tile([P, M, PACK], BF16)
-        table.append(wide_tile([P, T], I32))
+        w8_first = wide_tile([P, PACK, W8_CHUNK], F32)
+        table = [wide_tile([P, T], I32)]
+        grouped_first = wide_tile([P, W8_CHUNK, PACK], BF16)
+        table.extend(wide_tile([P, T], I32) for a in range(1, PASSES))
+        w8_rows = w8.rearrange("(p t) n -> p t n", t=PACK)
 
         def load_words(a):
             nc.sync.dma_start(out=table[a][:], in_=tab_words[a].rearrange("p t i -> p (t i)").bitcast(I32))
 
         for first, last, row in WINDOW_RUNS:
-            nc.sync.dma_start(out=scale_window[first:last, :], in_=table_scale_rows[row : row + last - first, :])
+            queue = nc.scalar if last - first == 20 else nc.sync
+            queue.dma_start(out=scale_window[first:last, :], in_=table_scale_rows[row : row + last - first, :])
         load_words(0)
         w4_scale_rows = w4_scales.bitcast(I32)
         for quad in range(QUADS):
@@ -95,8 +97,8 @@ def tile_list_tabgate_silu_kernel(
         nc.tensor.transpose(b_turned[:, 0:P], b_rows[:], ident[:])
         bias = keep.tile([P, ROW_TILES], F32, name="bias")
         nc.scalar.copy(out=bias[:], in_=b_turned[:, 0:ROW_TILES])
+        nc.sync.dma_start(out=w8_first[:], in_=w8_rows[:, :, 0:W8_CHUNK])
         load_words(1)
-        nc.sync.dma_start(out=w8_raw[:], in_=w8.rearrange("(p t) n -> p t n", t=PACK))
         load_words(2)
         w4_codes = keep.tile(
             [P, W4_PASSES, W4_WORD_BYTES * M // BYTES_PER_I32], I32, name="w4_codes", align_bytes=DMA_ALIGN
@@ -114,19 +116,21 @@ def tile_list_tabgate_silu_kernel(
                 in_=picked_scales[PASS2_AT[quad] : PASS2_AT[quad] + QUAD_BLOCKS, :].bitcast(I32),
             )
         w4_pass_planes = (picked_scales, pass2_plane)
-        for a in range(PASSES - 1):
-            nc.vector.tensor_copy(picked_words[a][:], table[a][:].bitcast(U32).indirect(offsets[:]))
+        nc.vector.tensor_copy(picked_words[0][:], table[0][:].bitcast(U32).indirect(offsets[:]))
 
         w8_codes = keep.tile([P, M], U32, name="w8_codes", align_bytes=MX_ALIGN)
         w8_plane = keep.tile([P, M], U8, name="w8_plane", align_bytes=MX_ALIGN)
-        for chunk in range(W8_CHUNKS):
-            features = slice(chunk * M // W8_CHUNKS, (chunk + 1) * M // W8_CHUNKS)
-            nc.scalar.copy(out=w8_grouped[:, features, :], in_=w8_raw[:, :, features].rearrange("p t n -> p n t"))
+
+        def quantise_w8(raw, grouped, features):
+            nc.scalar.copy(out=grouped[:], in_=raw[:].rearrange("p t n -> p n t"))
             nc.vector.quantize_mx(
                 out=w8_codes[:, features].bitcast(FP8X4),
                 scales=w8_plane[:, features],
-                in_=w8_grouped[:, features, :].rearrange("p n t -> p (n t)"),
+                in_=grouped[:].rearrange("p n t -> p (n t)"),
             )
+
+        quantise_w8(w8_first, grouped_first, slice(0, W8_CHUNK))
+        nc.vector.tensor_copy(picked_words[1][:], table[1][:].bitcast(U32).indirect(offsets[:]))
 
         for cols in token_slices:
             nc.vector.tensor_copy(picked_words[-1][:, cols], table[-1][:].bitcast(U32).indirect(entries(cols)))
@@ -136,10 +140,16 @@ def tile_list_tabgate_silu_kernel(
             gate_tile = wide_tile([P, T], F32)
             nc.sync.dma_start(out=gate_tile[:], in_=gT[i * P : (i + 1) * P, :])
             gate_tiles.append(gate_tile)
+            if i == 1:
+                w8_second = wide_tile([P, PACK, W8_CHUNK], F32)
+                nc.sync.dma_start(out=w8_second[:], in_=w8_rows[:, :, W8_CHUNK:M])
 
         for i in range(ROW_TILES):
             rows = slice(i * P, (i + 1) * P)
             gates = gate_tiles[i]
+            if i == 2:
+                grouped_second = keep.tile([P, W8_CHUNK, PACK], BF16, name="grouped_second", align_bytes=MX_ALIGN)
+                quantise_w8(w8_second, grouped_second, slice(W8_CHUNK, M))
             act = acts.tile([P, S], F32, name="act")
             for cols in token_slices:
                 acc = psum.tile([P, BANK], F32, name="acc", tag="acc")

@@ -32,9 +32,9 @@ QUAD_BLOCKS = 4
 MX_ALIGN = 64
 DMA_ALIGN = 256
 
-PASS0_SHIFT = 12
-WINDOW_RUNS = ((108, 128, 12), (12, 44, 0), (76, 108, 8), (44, 76, 4), (0, 4, 16), (4, 12, 40))
-PASS2_AT = (100, 104, 4, 8)
+PASS0_SHIFT = 4
+WINDOW_RUNS = ((0, 32, 0), (64, 80, 32))
+PASS_AT = (0, 16, 64)
 
 WIDE_SLOTS = 6
 ACT_SLOTS = 3
@@ -68,8 +68,6 @@ def tile_list_tabgate_silu_kernel(
         nc.vector.memset(w4_planes[:], 0)
         b_rows = keep.tile([P, P], F32, name="b_rows")
         nc.vector.memset(b_rows[:], 0.0)
-        ident = keep.tile([P, P], F32, name="ident")
-        make_identity(nc, ident[:])
 
         table_scale_rows = tab_scales.bitcast(I32).rearrange("a q t -> (a q) t")
         scale_window = wide_tile([P, T // BYTES_PER_I32], I32)
@@ -82,17 +80,17 @@ def tile_list_tabgate_silu_kernel(
         def load_words(a):
             nc.sync.dma_start(out=table[a][:], in_=tab_words[a].rearrange("p t i -> p (t i)").bitcast(I32))
 
+        nc.gpsimd.memset(scale_window[64:128, :], 0)
+        nc.vector.memset(scale_window[32:64, :], 0)
         for first, last, row in WINDOW_RUNS:
-            queue = nc.scalar if last - first == 20 else nc.sync
-            queue.dma_start(out=scale_window[first:last, :], in_=table_scale_rows[row : row + last - first, :])
+            nc.sync.dma_start(out=scale_window[first:last, :], in_=table_scale_rows[row : row + last - first, :])
         load_words(0)
-        w4_scale_rows = w4_scales.bitcast(I32)
-        for quad in range(QUADS):
-            nc.sync.dma_start(
-                out=w4_planes[QUAD * quad : QUAD * quad + QUAD_BLOCKS, :, :],
-                in_=w4_scale_rows[:, QUAD_BLOCKS * quad : QUAD_BLOCKS * (quad + 1), :].rearrange("a r n -> r a n"),
-            )
+        w4_scale_rows = w4_scales.bitcast(I32).rearrange("a (quad r) n -> r quad a n", r=QUAD_BLOCKS)
+        for r in range(QUAD_BLOCKS):
+            nc.sync.dma_start(out=w4_planes[r:P:QUAD, :, :], in_=w4_scale_rows[r])
         nc.sync.dma_start(out=b_rows[0:ROW_TILES, :], in_=b.rearrange("(i p) -> i p", p=P))
+        ident = keep.tile([P, P], F32, name="ident")
+        make_identity(nc, ident[:])
         b_turned = psum.tile([P, BANK], F32, name="acc", tag="acc")
         nc.tensor.transpose(b_turned[:, 0:P], b_rows[:], ident[:])
         bias = keep.tile([P, ROW_TILES], F32, name="bias")
@@ -107,15 +105,18 @@ def tile_list_tabgate_silu_kernel(
 
         picked_words = [keep.tile([P, S], U32, name=f"picked{a}", align_bytes=MX_ALIGN) for a in range(PASSES)]
         picked_scales = keep.tile([P, S], U8, name="planes0", align_bytes=MX_ALIGN)
+        planes01 = keep.tile([P, S], U8, name="planes01", align_bytes=MX_ALIGN)
         pass2_plane = keep.tile([P, S], U8, name="planes1", align_bytes=MX_ALIGN)
+        nc.gpsimd.memset(planes01[:].bitcast(I32), 0)
         nc.gpsimd.memset(pass2_plane[:].bitcast(I32), 0)
         nc.vector.tensor_copy(picked_scales[:], scale_window[:].bitcast(U8).indirect(offsets[:]))
-        for quad in range(QUADS):
-            nc.sync.dma_start(
-                out=pass2_plane[QUAD * quad : QUAD * quad + QUAD_BLOCKS, :].bitcast(I32),
-                in_=picked_scales[PASS2_AT[quad] : PASS2_AT[quad] + QUAD_BLOCKS, :].bitcast(I32),
-            )
-        w4_pass_planes = (picked_scales, pass2_plane)
+        for a, (plane, shift) in enumerate(((planes01, PASS0_SHIFT), (planes01, 0), (pass2_plane, 0))):
+            for r in range(QUAD_BLOCKS):
+                nc.gpsimd.dma_start(
+                    out=plane[shift + r : P : QUAD, :].bitcast(I32),
+                    in_=picked_scales[PASS_AT[a] + r : PASS_AT[a] + QUADS * QUAD_BLOCKS : QUAD_BLOCKS, :].bitcast(I32),
+                )
+        w4_pass_planes = (planes01, pass2_plane)
         nc.vector.tensor_copy(picked_words[0][:], table[0][:].bitcast(U32).indirect(offsets[:]))
 
         w8_codes = keep.tile([P, M], U32, name="w8_codes", align_bytes=MX_ALIGN)
@@ -158,7 +159,7 @@ def tile_list_tabgate_silu_kernel(
                     lhsT=w8_codes[:, rows].bitcast(FP8X4),
                     lhsT_scale=w8_plane[:, rows],
                     rhs=picked_words[0][:, cols].bitcast(FP8X4),
-                    rhs_scale=picked_scales[PASS0_SHIFT:P, cols],
+                    rhs_scale=planes01[PASS0_SHIFT:P, cols],
                     start=True,
                     stop=False,
                 )

@@ -34,13 +34,14 @@ DMA_ALIGN = 256
 
 PASS0_SHIFT = 4
 WINDOW_RUNS = ((0, 32, 0), (64, 80, 32))
+PASS_STEP = (1, 1, 2)
 PASS_AT = (0, 16, 64)
 
 WIDE_SLOTS = 6
 ACT_SLOTS = 3
 PSUM_BANKS = 8
 W8_CHUNK = M // 2
-LAST_TILE_PIECES = ((0, S // 2), (S // 2, 3 * S // 4), (3 * S // 4, S))
+LAST_TILE_PIECES = ((0, S // 2), (S // 2, 3 * S // 4), (3 * S // 4, S - P), (S - P, S))
 
 
 def tile_list_tabgate_silu_kernel(
@@ -58,6 +59,11 @@ def tile_list_tabgate_silu_kernel(
         def wide_tile(shape, dtype):
             return wide.tile(shape, dtype, name="wide_tile", tag="wide", align_bytes=DMA_ALIGN)
 
+        scale_window = wide_tile([P, T // BYTES_PER_I32], I32)
+        half = T // BYTES_PER_I32 // 2
+        nc.gpsimd.memset(scale_window[64:128, 0:half], 0)
+        nc.vector.memset(scale_window[64:128, half:], 0)
+        nc.vector.memset(scale_window[32:64, :], 0)
         offsets = keep.tile([P, S // STRIPE], U16, name="offsets")
         nc.sync.dma_start(offsets[:], offs)
 
@@ -70,7 +76,6 @@ def tile_list_tabgate_silu_kernel(
         nc.vector.memset(b_rows[:], 0.0)
 
         table_scale_rows = tab_scales.bitcast(I32).rearrange("a q t -> (a q) t")
-        scale_window = wide_tile([P, T // BYTES_PER_I32], I32)
         w8_first = wide_tile([P, PACK, W8_CHUNK], F32)
         table = [wide_tile([P, T], I32)]
         grouped_first = wide_tile([P, W8_CHUNK, PACK], BF16)
@@ -80,10 +85,8 @@ def tile_list_tabgate_silu_kernel(
         def load_words(a):
             nc.sync.dma_start(out=table[a][:], in_=tab_words[a].rearrange("p t i -> p (t i)").bitcast(I32))
 
-        nc.gpsimd.memset(scale_window[64:128, :], 0)
-        nc.vector.memset(scale_window[32:64, :], 0)
-        for first, last, row in WINDOW_RUNS:
-            nc.sync.dma_start(out=scale_window[first:last, :], in_=table_scale_rows[row : row + last - first, :])
+        nc.sync.dma_start(out=scale_window[0:32, :], in_=table_scale_rows[0:32, :])
+        nc.sync.dma_start(out=scale_window[64:96:2, :], in_=table_scale_rows[32:48, :])
         load_words(0)
         w4_scale_rows = w4_scales.bitcast(I32).rearrange("a (quad r) n -> r quad a n", r=QUAD_BLOCKS)
         for r in range(QUAD_BLOCKS):
@@ -114,7 +117,9 @@ def tile_list_tabgate_silu_kernel(
             for r in range(QUAD_BLOCKS):
                 nc.gpsimd.dma_start(
                     out=plane[shift + r : P : QUAD, :].bitcast(I32),
-                    in_=picked_scales[PASS_AT[a] + r : PASS_AT[a] + QUADS * QUAD_BLOCKS : QUAD_BLOCKS, :].bitcast(I32),
+                    in_=picked_scales[
+                        PASS_AT[a] + PASS_STEP[a] * r : PASS_AT[a] + PASS_STEP[a] * 16 : PASS_STEP[a] * QUAD_BLOCKS, :
+                    ].bitcast(I32),
                 )
         w4_pass_planes = (planes01, pass2_plane)
         nc.vector.tensor_copy(picked_words[0][:], table[0][:].bitcast(U32).indirect(offsets[:]))

@@ -40,7 +40,10 @@ PASS_AT = (0, 16, 64)
 WIDE_SLOTS = 6
 ACT_SLOTS = 3
 PSUM_BANKS = 8
-W8_CHUNK = M // 2
+W8_CHUNKS = 2
+HEAD_WORDS = T // 4
+EARLY_TILES = PSUM_BANKS * BANK // S
+W8_CHUNK = M // W8_CHUNKS
 LAST_TILE_PIECES = ((0, S // 2), (S // 2, 3 * S // 4), (3 * S // 4, S - P), (S - P, S))
 
 
@@ -76,18 +79,23 @@ def tile_list_tabgate_silu_kernel(
         nc.vector.memset(b_rows[:], 0.0)
 
         table_scale_rows = tab_scales.bitcast(I32).rearrange("a q t -> (a q) t")
-        w8_first = wide_tile([P, PACK, W8_CHUNK], F32)
+        w8_raw = wide_tile([P, W8_CHUNKS, PACK, W8_CHUNK], F32)
         table = [wide_tile([P, T], I32)]
-        grouped_first = wide_tile([P, W8_CHUNK, PACK], BF16)
+        w8_grouped = wide_tile([P, W8_CHUNKS, W8_CHUNK, PACK], BF16)
         table.extend(wide_tile([P, T], I32) for a in range(1, PASSES))
         w8_rows = w8.rearrange("(p t) n -> p t n", t=PACK)
 
-        def load_words(a):
-            nc.sync.dma_start(out=table[a][:], in_=tab_words[a].rearrange("p t i -> p (t i)").bitcast(I32))
+        def load_words(a, cols):
+            words = tab_words[a].rearrange("p t i -> p (t i)").bitcast(I32)
+            nc.sync.dma_start(out=table[a][:, cols], in_=words[:, cols])
+
+        def load_w8(h):
+            nc.sync.dma_start(out=w8_raw[:, h], in_=w8_rows[:, :, h * W8_CHUNK : (h + 1) * W8_CHUNK])
 
         nc.sync.dma_start(out=scale_window[0:32, :], in_=table_scale_rows[0:32, :])
+        load_words(0, slice(0, HEAD_WORDS))
         nc.sync.dma_start(out=scale_window[64:96:2, :], in_=table_scale_rows[32:48, :])
-        load_words(0)
+        load_words(0, slice(HEAD_WORDS, T))
         w4_scale_rows = w4_scales.bitcast(I32).rearrange("a (quad r) n -> r quad a n", r=QUAD_BLOCKS)
         for r in range(QUAD_BLOCKS):
             nc.sync.dma_start(out=w4_planes[r:P:QUAD, :, :], in_=w4_scale_rows[r])
@@ -98,9 +106,10 @@ def tile_list_tabgate_silu_kernel(
         nc.tensor.transpose(b_turned[:, 0:P], b_rows[:], ident[:])
         bias = keep.tile([P, ROW_TILES], F32, name="bias")
         nc.scalar.copy(out=bias[:], in_=b_turned[:, 0:ROW_TILES])
-        nc.sync.dma_start(out=w8_first[:], in_=w8_rows[:, :, 0:W8_CHUNK])
-        load_words(1)
-        load_words(2)
+        load_w8(0)
+        load_words(1, slice(0, T))
+        load_w8(1)
+        load_words(2, slice(0, T))
         w4_codes = keep.tile(
             [P, W4_PASSES, W4_WORD_BYTES * M // BYTES_PER_I32], I32, name="w4_codes", align_bytes=DMA_ALIGN
         )
@@ -127,16 +136,18 @@ def tile_list_tabgate_silu_kernel(
         w8_codes = keep.tile([P, M], U32, name="w8_codes", align_bytes=MX_ALIGN)
         w8_plane = keep.tile([P, M], U8, name="w8_plane", align_bytes=MX_ALIGN)
 
-        def quantise_w8(raw, grouped, features):
-            nc.scalar.copy(out=grouped[:], in_=raw[:].rearrange("p t n -> p n t"))
+        def quantise_w8(h):
+            features = slice(h * W8_CHUNK, (h + 1) * W8_CHUNK)
+            nc.scalar.copy(out=w8_grouped[:, h], in_=w8_raw[:, h].rearrange("p t n -> p n t"))
             nc.vector.quantize_mx(
                 out=w8_codes[:, features].bitcast(FP8X4),
                 scales=w8_plane[:, features],
-                in_=grouped[:].rearrange("p n t -> p (n t)"),
+                in_=w8_grouped[:, h].rearrange("p n t -> p (n t)"),
             )
 
-        quantise_w8(w8_first, grouped_first, slice(0, W8_CHUNK))
+        quantise_w8(0)
         nc.vector.tensor_copy(picked_words[1][:], table[1][:].bitcast(U32).indirect(offsets[:]))
+        quantise_w8(1)
 
         for cols in token_slices:
             nc.vector.tensor_copy(picked_words[-1][:, cols], table[-1][:].bitcast(U32).indirect(entries(cols)))
@@ -146,40 +157,51 @@ def tile_list_tabgate_silu_kernel(
             gate_tile = wide_tile([P, T], F32)
             nc.sync.dma_start(out=gate_tile[:], in_=gT[i * P : (i + 1) * P, :])
             gate_tiles.append(gate_tile)
-            if i == 1:
-                w8_second = wide_tile([P, PACK, W8_CHUNK], F32)
-                nc.sync.dma_start(out=w8_second[:], in_=w8_rows[:, :, W8_CHUNK:M])
+
+        def mx_pass(acc, a, i, cols):
+            rows = slice(i * P, (i + 1) * P)
+            if a == 0:
+                codes, scales = w8_codes[:, rows].bitcast(FP8X4), w8_plane[:, rows]
+                table_plane = planes01[PASS0_SHIFT:P, cols]
+            else:
+                w4_bytes = slice(W4_WORD_BYTES * rows.start, W4_WORD_BYTES * rows.stop)
+                codes = w4_codes[:, a - 1, :].bitcast(U8)[:, w4_bytes].bitcast(FP4X4)
+                scales = w4_planes[:, a - 1, :].bitcast(U8)[:, rows]
+                table_plane = w4_pass_planes[a - 1][:, cols]
+            nc.tensor.matmul_mx(
+                out=acc[:],
+                lhsT=codes,
+                lhsT_scale=scales,
+                rhs=picked_words[a][:, cols].bitcast(FP8X4),
+                rhs_scale=table_plane,
+                start=(a == 0),
+                stop=(a == PASSES - 1),
+            )
+
+        def silu_out(act, acc, i, cols):
+            nc.scalar.activation(out=act[:, cols], in_=acc[:], func=SILU, bias=bias[:, i : i + 1])
+
+        early = [(i, cols) for cols in token_slices for i in range(EARLY_TILES)]
+        early_accs = [psum.tile([P, BANK], F32, name="acc", tag="acc") for unit in early]
+        early_acts = [acts.tile([P, S], F32, name="act") for i in range(EARLY_TILES)]
+        for a in range(PASSES):
+            for acc, (i, cols) in zip(early_accs, early):
+                mx_pass(acc, a, i, cols)
+                if a == PASSES - 1:
+                    silu_out(early_acts[i], acc, i, cols)
 
         for i in range(ROW_TILES):
             rows = slice(i * P, (i + 1) * P)
             gates = gate_tiles[i]
-            if i == 2:
-                grouped_second = keep.tile([P, W8_CHUNK, PACK], BF16, name="grouped_second", align_bytes=MX_ALIGN)
-                quantise_w8(w8_second, grouped_second, slice(W8_CHUNK, M))
-            act = acts.tile([P, S], F32, name="act")
-            for cols in token_slices:
-                acc = psum.tile([P, BANK], F32, name="acc", tag="acc")
-                nc.tensor.matmul_mx(
-                    out=acc[:],
-                    lhsT=w8_codes[:, rows].bitcast(FP8X4),
-                    lhsT_scale=w8_plane[:, rows],
-                    rhs=picked_words[0][:, cols].bitcast(FP8X4),
-                    rhs_scale=planes01[PASS0_SHIFT:P, cols],
-                    start=True,
-                    stop=False,
-                )
-                for c in range(W4_PASSES):
-                    w4_bytes = slice(W4_WORD_BYTES * rows.start, W4_WORD_BYTES * rows.stop)
-                    nc.tensor.matmul_mx(
-                        out=acc[:],
-                        lhsT=w4_codes[:, c, :].bitcast(U8)[:, w4_bytes].bitcast(FP4X4),
-                        lhsT_scale=w4_planes[:, c, :].bitcast(U8)[:, rows],
-                        rhs=picked_words[1 + c][:, cols].bitcast(FP8X4),
-                        rhs_scale=w4_pass_planes[c][:, cols],
-                        start=False,
-                        stop=(c == W4_PASSES - 1),
-                    )
-                nc.scalar.activation(out=act[:, cols], in_=acc[:], func=SILU, bias=bias[:, i : i + 1])
+            if i < EARLY_TILES:
+                act = early_acts[i]
+            else:
+                act = acts.tile([P, S], F32, name="act")
+                for cols in token_slices:
+                    acc = psum.tile([P, BANK], F32, name="acc", tag="acc")
+                    for a in range(PASSES):
+                        mx_pass(acc, a, i, cols)
+                    silu_out(act, acc, i, cols)
 
             if i % 2 == 0:
                 result_pair = results.tile([P, 2, S], F32, name="result_pair", align_bytes=DMA_ALIGN)

@@ -32,10 +32,9 @@ QUAD_BLOCKS = 4
 MX_ALIGN = 64
 DMA_ALIGN = 256
 
-PASS0_SHIFT = 4
-WINDOW_RUNS = ((0, 32, 0), (64, 80, 32))
-PASS_STEP = (1, 1, 2)
-PASS_AT = (0, 16, 64)
+PASS0_SHIFT = 8
+WINDOW_AT = 4
+WINDOW_STEP = 8
 
 WIDE_SLOTS = 6
 ACT_SLOTS = 3
@@ -64,11 +63,9 @@ def tile_list_tabgate_silu_kernel(
 
         scale_window = wide_tile([P, T // BYTES_PER_I32], I32)
         half = T // BYTES_PER_I32 // 2
-        nc.gpsimd.memset(scale_window[64:128, 0:half], 0)
-        nc.vector.memset(scale_window[64:128, half:], 0)
-        nc.vector.memset(scale_window[32:64, :], 0)
+        nc.gpsimd.memset(scale_window[:, 0:half], 0)
+        nc.vector.memset(scale_window[:, half:], 0)
         offsets = keep.tile([P, S // STRIPE], U16, name="offsets")
-        nc.sync.dma_start(offsets[:], offs)
 
         def entries(cols):
             return offsets[:, cols.start // STRIPE : cols.stop // STRIPE]
@@ -78,7 +75,7 @@ def tile_list_tabgate_silu_kernel(
         b_rows = keep.tile([P, P], F32, name="b_rows")
         nc.vector.memset(b_rows[:], 0.0)
 
-        table_scale_rows = tab_scales.bitcast(I32).rearrange("a q t -> (a q) t")
+        table_scale_rows = tab_scales.bitcast(I32)
         w8_raw = wide_tile([P, W8_CHUNKS, PACK, W8_CHUNK], F32)
         table = [wide_tile([P, T], I32)]
         w8_grouped = wide_tile([P, W8_CHUNKS, W8_CHUNK, PACK], BF16)
@@ -92,9 +89,10 @@ def tile_list_tabgate_silu_kernel(
         def load_w8(h):
             nc.sync.dma_start(out=w8_raw[:, h], in_=w8_rows[:, :, h * W8_CHUNK : (h + 1) * W8_CHUNK])
 
-        nc.sync.dma_start(out=scale_window[0:32, :], in_=table_scale_rows[0:32, :])
         load_words(0, slice(0, HEAD_WORDS))
-        nc.sync.dma_start(out=scale_window[64:96:2, :], in_=table_scale_rows[32:48, :])
+        nc.sync.dma_start(offsets[:], offs)
+        for a in range(PASSES):
+            nc.sync.dma_start(out=scale_window[WINDOW_AT + a : P : WINDOW_STEP, :], in_=table_scale_rows[a])
         load_words(0, slice(HEAD_WORDS, T))
         w4_scale_rows = w4_scales.bitcast(I32).rearrange("a (quad r) n -> r quad a n", r=QUAD_BLOCKS)
         for r in range(QUAD_BLOCKS):
@@ -126,9 +124,7 @@ def tile_list_tabgate_silu_kernel(
             for r in range(QUAD_BLOCKS):
                 nc.gpsimd.dma_start(
                     out=plane[shift + r : P : QUAD, :].bitcast(I32),
-                    in_=picked_scales[
-                        PASS_AT[a] + PASS_STEP[a] * r : PASS_AT[a] + PASS_STEP[a] * 16 : PASS_STEP[a] * QUAD_BLOCKS, :
-                    ].bitcast(I32),
+                    in_=picked_scales[WINDOW_AT + a + WINDOW_STEP * r : P : QUAD, :].bitcast(I32),
                 )
         w4_pass_planes = (planes01, pass2_plane)
         nc.vector.tensor_copy(picked_words[0][:], table[0][:].bitcast(U32).indirect(offsets[:]))

@@ -40,7 +40,7 @@ WIDE_SLOTS = 6
 ACT_SLOTS = 3
 PSUM_BANKS = 8
 W8_CHUNKS = 2
-HEAD_WORDS = T // 4
+HEAD_WORDS = T // 2
 EARLY_TILES = PSUM_BANKS * BANK // S
 W8_CHUNK = M // W8_CHUNKS
 LAST_TILE_PIECES = ((0, S // 2), (S // 2, 3 * S // 4), (3 * S // 4, S - P), (S - P, S))

@@ -33,8 +33,8 @@ MX_ALIGN = 64
 DMA_ALIGN = 256
 
 PASS0_SHIFT = 8
-WINDOW_AT = 4
-WINDOW_STEP = 8
+WINDOW_AT = (32, 64, 33)
+WINDOW_STEP = (2, 2, 4)
 
 WIDE_SLOTS = 6
 ACT_SLOTS = 3
@@ -75,7 +75,7 @@ def tile_list_tabgate_silu_kernel(
         b_rows = keep.tile([P, P], F32, name="b_rows")
         nc.vector.memset(b_rows[:], 0.0)
 
-        table_scale_rows = tab_scales.bitcast(I32)
+        table_scale_rows = tab_scales.bitcast(I32).rearrange("a q t -> (a q) t")
         w8_raw = wide_tile([P, W8_CHUNKS, PACK, W8_CHUNK], F32)
         table = [wide_tile([P, T], I32)]
         w8_grouped = wide_tile([P, W8_CHUNKS, W8_CHUNK, PACK], BF16)
@@ -91,8 +91,8 @@ def tile_list_tabgate_silu_kernel(
 
         load_words(0, slice(0, HEAD_WORDS))
         nc.sync.dma_start(offsets[:], offs)
-        for a in range(PASSES):
-            nc.sync.dma_start(out=scale_window[WINDOW_AT + a : P : WINDOW_STEP, :], in_=table_scale_rows[a])
+        nc.sync.dma_start(out=scale_window[32:96:2, :], in_=table_scale_rows[0:32, :])
+        nc.sync.dma_start(out=scale_window[33:96:4, :], in_=table_scale_rows[32:48, :])
         load_words(0, slice(HEAD_WORDS, T))
         w4_scale_rows = w4_scales.bitcast(I32).rearrange("a (quad r) n -> r quad a n", r=QUAD_BLOCKS)
         for r in range(QUAD_BLOCKS):
@@ -124,7 +124,9 @@ def tile_list_tabgate_silu_kernel(
             for r in range(QUAD_BLOCKS):
                 nc.gpsimd.dma_start(
                     out=plane[shift + r : P : QUAD, :].bitcast(I32),
-                    in_=picked_scales[WINDOW_AT + a + WINDOW_STEP * r : P : QUAD, :].bitcast(I32),
+                    in_=picked_scales[
+                        WINDOW_AT[a] + WINDOW_STEP[a] * r : WINDOW_AT[a] + WINDOW_STEP[a] * 16 : WINDOW_STEP[a] * QUAD_BLOCKS, :
+                    ].bitcast(I32),
                 )
         w4_pass_planes = (planes01, pass2_plane)
         nc.vector.tensor_copy(picked_words[0][:], table[0][:].bitcast(U32).indirect(offsets[:]))

@@ -32,18 +32,17 @@ QUAD_BLOCKS = 4
 MX_ALIGN = 64
 DMA_ALIGN = 256
 
-PASS0_SHIFT = 8
+PASS0_SHIFT = 4
 WINDOW_AT = (32, 64, 33)
 WINDOW_STEP = (2, 2, 4)
 
-WIDE_SLOTS = 6
+WIDE_SLOTS = 5
 ACT_SLOTS = 3
 PSUM_BANKS = 8
 W8_CHUNKS = 2
-HEAD_WORDS = T // 2
 EARLY_TILES = PSUM_BANKS * BANK // S
 W8_CHUNK = M // W8_CHUNKS
-LAST_TILE_PIECES = ((0, S // 2), (S // 2, 3 * S // 4), (3 * S // 4, S - P), (S - P, S))
+STORE_FROM = {4: 0, 6: 4, 7: 6, 8: 7}
 
 
 def tile_list_tabgate_silu_kernel(
@@ -54,7 +53,7 @@ def tile_list_tabgate_silu_kernel(
     with ExitStack() as ctx:
         keep = ctx.enter_context(tc.tile_pool(name="keep", bufs=1))
         wide = ctx.enter_context(tc.tile_pool(name="wide", bufs=WIDE_SLOTS))
-        results = ctx.enter_context(tc.tile_pool(name="results", bufs=ROW_TILES // 2))
+        results = ctx.enter_context(tc.tile_pool(name="results", bufs=1))
         acts = ctx.enter_context(tc.tile_pool(name="acts", bufs=ACT_SLOTS))
         psum = ctx.enter_context(tc.psum_pool(name="psum", bufs=PSUM_BANKS))
 
@@ -76,9 +75,9 @@ def tile_list_tabgate_silu_kernel(
         nc.vector.memset(b_rows[:], 0.0)
 
         table_scale_rows = tab_scales.bitcast(I32).rearrange("a q t -> (a q) t")
-        w8_raw = wide_tile([P, W8_CHUNKS, PACK, W8_CHUNK], F32)
+        w8_raw = wide_tile([P, PACK, M], F32)
         table = [wide_tile([P, T], I32)]
-        w8_grouped = wide_tile([P, W8_CHUNKS, W8_CHUNK, PACK], BF16)
+        w8_grouped = keep.tile([P, W8_CHUNKS, W8_CHUNK, PACK], BF16, name="w8_grouped", tag="reused", align_bytes=MX_ALIGN)
         table.extend(wide_tile([P, T], I32) for a in range(1, PASSES))
         w8_rows = w8.rearrange("(p t) n -> p t n", t=PACK)
 
@@ -86,14 +85,14 @@ def tile_list_tabgate_silu_kernel(
             words = tab_words[a].rearrange("p t i -> p (t i)").bitcast(I32)
             nc.sync.dma_start(out=table[a][:, cols], in_=words[:, cols])
 
-        def load_w8(h):
-            nc.sync.dma_start(out=w8_raw[:, h], in_=w8_rows[:, :, h * W8_CHUNK : (h + 1) * W8_CHUNK])
-
-        load_words(0, slice(0, HEAD_WORDS))
+        w4_codes = keep.tile(
+            [P, W4_PASSES, W4_WORD_BYTES * M // BYTES_PER_I32], I32, name="w4_codes", align_bytes=DMA_ALIGN
+        )
+        nc.sync.dma_start(out=w4_codes[:], in_=w4_words.bitcast(I32).rearrange("a p n -> p a n"))
         nc.sync.dma_start(offsets[:], offs)
         nc.sync.dma_start(out=scale_window[32:96:2, :], in_=table_scale_rows[0:32, :])
         nc.sync.dma_start(out=scale_window[33:96:4, :], in_=table_scale_rows[32:48, :])
-        load_words(0, slice(HEAD_WORDS, T))
+        load_words(0, slice(0, T))
         w4_scale_rows = w4_scales.bitcast(I32).rearrange("a (quad r) n -> r quad a n", r=QUAD_BLOCKS)
         for r in range(QUAD_BLOCKS):
             nc.sync.dma_start(out=w4_planes[r:P:QUAD, :, :], in_=w4_scale_rows[r])
@@ -104,31 +103,39 @@ def tile_list_tabgate_silu_kernel(
         nc.tensor.transpose(b_turned[:, 0:P], b_rows[:], ident[:])
         bias = keep.tile([P, ROW_TILES], F32, name="bias")
         nc.scalar.copy(out=bias[:], in_=b_turned[:, 0:ROW_TILES])
-        load_w8(0)
+        nc.sync.dma_start(out=w8_raw[:], in_=w8_rows)
         load_words(1, slice(0, T))
-        load_w8(1)
         load_words(2, slice(0, T))
-        w4_codes = keep.tile(
-            [P, W4_PASSES, W4_WORD_BYTES * M // BYTES_PER_I32], I32, name="w4_codes", align_bytes=DMA_ALIGN
-        )
-        nc.sync.dma_start(out=w4_codes[:], in_=w4_words.bitcast(I32).rearrange("a p n -> p a n"))
 
-        picked_words = [keep.tile([P, S], U32, name=f"picked{a}", align_bytes=MX_ALIGN) for a in range(PASSES)]
+        picked_words = {a: keep.tile([P, S], U32, name=f"picked{a}", align_bytes=MX_ALIGN) for a in (0, 2)}
         picked_scales = keep.tile([P, S], U8, name="planes0", align_bytes=MX_ALIGN)
-        planes01 = keep.tile([P, S], U8, name="planes01", align_bytes=MX_ALIGN)
-        pass2_plane = keep.tile([P, S], U8, name="planes1", align_bytes=MX_ALIGN)
-        nc.gpsimd.memset(planes01[:].bitcast(I32), 0)
-        nc.gpsimd.memset(pass2_plane[:].bitcast(I32), 0)
+        planes = [keep.tile([P, S], U8, name=f"plane{a}", align_bytes=MX_ALIGN) for a in range(PASSES)]
+        for plane in planes:
+            nc.gpsimd.memset(plane[:].bitcast(I32), 0)
         nc.vector.tensor_copy(picked_scales[:], scale_window[:].bitcast(U8).indirect(offsets[:]))
-        for a, (plane, shift) in enumerate(((planes01, PASS0_SHIFT), (planes01, 0), (pass2_plane, 0))):
-            for r in range(QUAD_BLOCKS):
-                nc.gpsimd.dma_start(
-                    out=plane[shift + r : P : QUAD, :].bitcast(I32),
-                    in_=picked_scales[
-                        WINDOW_AT[a] + WINDOW_STEP[a] * r : WINDOW_AT[a] + WINDOW_STEP[a] * 16 : WINDOW_STEP[a] * QUAD_BLOCKS, :
-                    ].bitcast(I32),
-                )
-        w4_pass_planes = (planes01, pass2_plane)
+
+        def move_scale_rows(a, r):
+            shift = PASS0_SHIFT if a == 0 else 0
+            first = WINDOW_AT[a] + WINDOW_STEP[a] * r
+            stop = WINDOW_AT[a] + WINDOW_STEP[a] * QUADS * QUAD_BLOCKS
+            nc.sync.dma_start(
+                out=planes[a][shift + r : P : QUAD, :].bitcast(I32),
+                in_=picked_scales[first : stop : WINDOW_STEP[a] * QUAD_BLOCKS, :].bitcast(I32),
+            )
+
+        gate_tiles = []
+
+        def load_gates(i):
+            gate_tile = wide_tile([P, T], F32)
+            nc.sync.dma_start(out=gate_tile[:], in_=gT[i * P : (i + 1) * P, :])
+            gate_tiles.append(gate_tile)
+
+        moves = [(a, r) for a in range(PASSES) for r in range(QUAD_BLOCKS)]
+        for a, r in moves[: len(moves) // 2]:
+            move_scale_rows(a, r)
+        load_gates(0)
+        for a, r in moves[len(moves) // 2 :]:
+            move_scale_rows(a, r)
         nc.vector.tensor_copy(picked_words[0][:], table[0][:].bitcast(U32).indirect(offsets[:]))
 
         w8_codes = keep.tile([P, M], U32, name="w8_codes", align_bytes=MX_ALIGN)
@@ -136,7 +143,7 @@ def tile_list_tabgate_silu_kernel(
 
         def quantise_w8(h):
             features = slice(h * W8_CHUNK, (h + 1) * W8_CHUNK)
-            nc.scalar.copy(out=w8_grouped[:, h], in_=w8_raw[:, h].rearrange("p t n -> p n t"))
+            nc.scalar.copy(out=w8_grouped[:, h], in_=w8_raw[:, :, features].rearrange("p t n -> p n t"))
             nc.vector.quantize_mx(
                 out=w8_codes[:, features].bitcast(FP8X4),
                 scales=w8_plane[:, features],
@@ -144,28 +151,26 @@ def tile_list_tabgate_silu_kernel(
             )
 
         quantise_w8(0)
-        nc.vector.tensor_copy(picked_words[1][:], table[1][:].bitcast(U32).indirect(offsets[:]))
         quantise_w8(1)
+        picked_words[1] = keep.tile([P, S], U32, name="picked1", tag="reused", align_bytes=MX_ALIGN)
+        nc.vector.tensor_copy(picked_words[1][:], table[1][:].bitcast(U32).indirect(offsets[:]))
 
         for cols in token_slices:
-            nc.vector.tensor_copy(picked_words[-1][:, cols], table[-1][:].bitcast(U32).indirect(entries(cols)))
+            nc.vector.tensor_copy(picked_words[PASSES - 1][:, cols], table[-1][:].bitcast(U32).indirect(entries(cols)))
 
-        gate_tiles = []
-        for i in range(ROW_TILES):
-            gate_tile = wide_tile([P, T], F32)
-            nc.sync.dma_start(out=gate_tile[:], in_=gT[i * P : (i + 1) * P, :])
-            gate_tiles.append(gate_tile)
+        for i in range(1, ROW_TILES):
+            load_gates(i)
 
         def mx_pass(acc, a, i, cols):
             rows = slice(i * P, (i + 1) * P)
             if a == 0:
                 codes, scales = w8_codes[:, rows].bitcast(FP8X4), w8_plane[:, rows]
-                table_plane = planes01[PASS0_SHIFT:P, cols]
+                table_plane = planes[0][PASS0_SHIFT:P, cols]
             else:
                 w4_bytes = slice(W4_WORD_BYTES * rows.start, W4_WORD_BYTES * rows.stop)
                 codes = w4_codes[:, a - 1, :].bitcast(U8)[:, w4_bytes].bitcast(FP4X4)
                 scales = w4_planes[:, a - 1, :].bitcast(U8)[:, rows]
-                table_plane = w4_pass_planes[a - 1][:, cols]
+                table_plane = planes[a][:, cols]
             nc.tensor.matmul_mx(
                 out=acc[:],
                 lhsT=codes,
@@ -188,8 +193,8 @@ def tile_list_tabgate_silu_kernel(
                 if a == PASSES - 1:
                     silu_out(early_acts[i], acc, i, cols)
 
+        result_all = results.tile([P, ROW_TILES, S], F32, name="result_all", align_bytes=DMA_ALIGN)
         for i in range(ROW_TILES):
-            rows = slice(i * P, (i + 1) * P)
             gates = gate_tiles[i]
             if i < EARLY_TILES:
                 act = early_acts[i]
@@ -201,22 +206,13 @@ def tile_list_tabgate_silu_kernel(
                         mx_pass(acc, a, i, cols)
                     silu_out(act, acc, i, cols)
 
-            if i % 2 == 0:
-                result_pair = results.tile([P, 2, S], F32, name="result_pair", align_bytes=DMA_ALIGN)
-            result = result_pair[:, i % 2, :]
-            if i == ROW_TILES - 1:
-                for first, last in LAST_TILE_PIECES:
-                    cols = slice(first, last)
-                    nc.vector.tensor_tensor(result[:, cols], gates[:].indirect(entries(cols)), act[:, cols], MULT)
-                    nc.sync.dma_start(out=out[rows, cols], in_=result[:, cols])
-                continue
+            result = result_all[:, i, :]
             if i == 0:
                 for cols in token_slices:
                     nc.vector.tensor_tensor(result[:, cols], gates[:].indirect(entries(cols)), act[:, cols], MULT)
             else:
                 nc.vector.tensor_tensor(result, gates[:].indirect(offsets[:]), act[:], MULT)
-            if i == ROW_TILES - 2:
-                nc.sync.dma_start(out=out[rows, :], in_=result)
-            elif i % 2 == 1:
-                pair_rows = out[(i - 1) * P : (i + 1) * P, :].rearrange("(h p) j -> p h j", p=P)
-                nc.sync.dma_start(out=pair_rows, in_=result_pair[:])
+            if i + 1 in STORE_FROM:
+                first = STORE_FROM[i + 1]
+                stored_rows = out[first * P : (i + 1) * P, :].rearrange("(h p) j -> p h j", p=P)
+                nc.sync.dma_start(out=stored_rows, in_=result_all[:, first : i + 1, :])

@@ -42,7 +42,8 @@ PSUM_BANKS = 8
 W8_CHUNKS = 2
 EARLY_TILES = PSUM_BANKS * BANK // S
 W8_CHUNK = M // W8_CHUNKS
-STORE_FROM = {4: 0, 6: 4, 7: 6, 8: 7}
+STORE_FROM = {4: 0, 6: 4, 7: 6}
+LAST_TILE_PIECES = ((0, 1024), (1024, 1792), (1792, 2048))
 
 
 def tile_list_tabgate_silu_kernel(
@@ -92,7 +93,7 @@ def tile_list_tabgate_silu_kernel(
         nc.sync.dma_start(offsets[:], offs)
         nc.sync.dma_start(out=scale_window[32:96:2, :], in_=table_scale_rows[0:32, :])
         nc.sync.dma_start(out=scale_window[33:96:4, :], in_=table_scale_rows[32:48, :])
-        load_words(0, slice(0, T))
+        nc.sync.dma_start(out=w8_raw[:], in_=w8_rows)
         w4_scale_rows = w4_scales.bitcast(I32).rearrange("a (quad r) n -> r quad a n", r=QUAD_BLOCKS)
         for r in range(QUAD_BLOCKS):
             nc.sync.dma_start(out=w4_planes[r:P:QUAD, :, :], in_=w4_scale_rows[r])
@@ -103,7 +104,7 @@ def tile_list_tabgate_silu_kernel(
         nc.tensor.transpose(b_turned[:, 0:P], b_rows[:], ident[:])
         bias = keep.tile([P, ROW_TILES], F32, name="bias")
         nc.scalar.copy(out=bias[:], in_=b_turned[:, 0:ROW_TILES])
-        nc.sync.dma_start(out=w8_raw[:], in_=w8_rows)
+        load_words(0, slice(0, T))
         load_words(1, slice(0, T))
         load_words(2, slice(0, T))
 
@@ -118,7 +119,8 @@ def tile_list_tabgate_silu_kernel(
             shift = PASS0_SHIFT if a == 0 else 0
             first = WINDOW_AT[a] + WINDOW_STEP[a] * r
             stop = WINDOW_AT[a] + WINDOW_STEP[a] * QUADS * QUAD_BLOCKS
-            nc.sync.dma_start(
+            queue = nc.sync if a == PASSES - 1 else nc.gpsimd
+            queue.dma_start(
                 out=planes[a][shift + r : P : QUAD, :].bitcast(I32),
                 in_=picked_scales[first : stop : WINDOW_STEP[a] * QUAD_BLOCKS, :].bitcast(I32),
             )
@@ -131,11 +133,9 @@ def tile_list_tabgate_silu_kernel(
             gate_tiles.append(gate_tile)
 
         moves = [(a, r) for a in range(PASSES) for r in range(QUAD_BLOCKS)]
-        for a, r in moves[: len(moves) // 2]:
+        for a, r in moves:
             move_scale_rows(a, r)
         load_gates(0)
-        for a, r in moves[len(moves) // 2 :]:
-            move_scale_rows(a, r)
         nc.vector.tensor_copy(picked_words[0][:], table[0][:].bitcast(U32).indirect(offsets[:]))
 
         w8_codes = keep.tile([P, M], U32, name="w8_codes", align_bytes=MX_ALIGN)
@@ -143,7 +143,10 @@ def tile_list_tabgate_silu_kernel(
 
         def quantise_w8(h):
             features = slice(h * W8_CHUNK, (h + 1) * W8_CHUNK)
-            nc.scalar.copy(out=w8_grouped[:, h], in_=w8_raw[:, :, features].rearrange("p t n -> p n t"))
+            nc.scalar.copy(
+                out=w8_grouped[:, h].rearrange("p (c i) t -> p c t i", i=PACK),
+                in_=w8_raw[:, :, features].rearrange("p t (c i) -> p c t i", i=PACK),
+            )
             nc.vector.quantize_mx(
                 out=w8_codes[:, features].bitcast(FP8X4),
                 scales=w8_plane[:, features],
@@ -207,7 +210,12 @@ def tile_list_tabgate_silu_kernel(
                     silu_out(act, acc, i, cols)
 
             result = result_all[:, i, :]
-            if i == 0:
+            if i == ROW_TILES - 1:
+                for first, last in LAST_TILE_PIECES:
+                    cols = slice(first, last)
+                    nc.vector.tensor_tensor(result[:, cols], gates[:].indirect(entries(cols)), act[:, cols], MULT)
+                    nc.sync.dma_start(out=out[i * P : (i + 1) * P, cols], in_=result[:, cols])
+            elif i == 0:
                 for cols in token_slices:
                     nc.vector.tensor_tensor(result[:, cols], gates[:].indirect(entries(cols)), act[:, cols], MULT)
             else:

@@ -36,7 +36,7 @@ PASS0_SHIFT = 4
 WINDOW_AT = (32, 64, 33)
 WINDOW_STEP = (2, 2, 4)
 
-WIDE_SLOTS = 5
+WIDE_SLOTS = 6
 ACT_SLOTS = 3
 PSUM_BANKS = 8
 W8_CHUNKS = 2
@@ -62,9 +62,7 @@ def tile_list_tabgate_silu_kernel(
             return wide.tile(shape, dtype, name="wide_tile", tag="wide", align_bytes=DMA_ALIGN)
 
         scale_window = wide_tile([P, T // BYTES_PER_I32], I32)
-        half = T // BYTES_PER_I32 // 2
-        nc.gpsimd.memset(scale_window[:, 0:half], 0)
-        nc.vector.memset(scale_window[:, half:], 0)
+        nc.vector.memset(scale_window[:], 0)
         offsets = keep.tile([P, S // STRIPE], U16, name="offsets")
 
         def entries(cols):
@@ -93,18 +91,19 @@ def tile_list_tabgate_silu_kernel(
         nc.sync.dma_start(offsets[:], offs)
         nc.sync.dma_start(out=scale_window[32:96:2, :], in_=table_scale_rows[0:32, :])
         nc.sync.dma_start(out=scale_window[33:96:4, :], in_=table_scale_rows[32:48, :])
-        nc.sync.dma_start(out=w8_raw[:], in_=w8_rows)
+        load_words(0, slice(0, T))
         w4_scale_rows = w4_scales.bitcast(I32).rearrange("a (quad r) n -> r quad a n", r=QUAD_BLOCKS)
         for r in range(QUAD_BLOCKS):
             nc.sync.dma_start(out=w4_planes[r:P:QUAD, :, :], in_=w4_scale_rows[r])
         nc.sync.dma_start(out=b_rows[0:ROW_TILES, :], in_=b.rearrange("(i p) -> i p", p=P))
         ident = keep.tile([P, P], F32, name="ident")
-        make_identity(nc, ident[:])
+        nc.vector.memset(ident[:], 0.0)
+        make_identity(nc, ident[:], nomemset=True)
         b_turned = psum.tile([P, BANK], F32, name="acc", tag="acc")
         nc.tensor.transpose(b_turned[:, 0:P], b_rows[:], ident[:])
         bias = keep.tile([P, ROW_TILES], F32, name="bias")
         nc.scalar.copy(out=bias[:], in_=b_turned[:, 0:ROW_TILES])
-        load_words(0, slice(0, T))
+        nc.sync.dma_start(out=w8_raw[:], in_=w8_rows)
         load_words(1, slice(0, T))
         load_words(2, slice(0, T))
 
@@ -112,7 +111,7 @@ def tile_list_tabgate_silu_kernel(
         picked_scales = keep.tile([P, S], U8, name="planes0", align_bytes=MX_ALIGN)
         planes = [keep.tile([P, S], U8, name=f"plane{a}", align_bytes=MX_ALIGN) for a in range(PASSES)]
         for plane in planes:
-            nc.gpsimd.memset(plane[:].bitcast(I32), 0)
+            nc.vector.memset(plane[:].bitcast(I32), 0)
         nc.vector.tensor_copy(picked_scales[:], scale_window[:].bitcast(U8).indirect(offsets[:]))
 
         def move_scale_rows(a, r):
@@ -133,9 +132,9 @@ def tile_list_tabgate_silu_kernel(
             gate_tiles.append(gate_tile)
 
         moves = [(a, r) for a in range(PASSES) for r in range(QUAD_BLOCKS)]
+        load_gates(0)
         for a, r in moves:
             move_scale_rows(a, r)
-        load_gates(0)
         nc.vector.tensor_copy(picked_words[0][:], table[0][:].bitcast(U32).indirect(offsets[:]))
 
         w8_codes = keep.tile([P, M], U32, name="w8_codes", align_bytes=MX_ALIGN)

@@ -33,6 +33,8 @@ MX_ALIGN = 64
 DMA_ALIGN = 256
 
 PASS0_SHIFT = 4
+PASS_ORDER = (1, 2, 0)
+B_AT = 16
 WINDOW_AT = (32, 64, 33)
 WINDOW_STEP = (2, 2, 4)
 
@@ -74,10 +76,13 @@ def tile_list_tabgate_silu_kernel(
         nc.vector.memset(b_rows[:], 0.0)
 
         table_scale_rows = tab_scales.bitcast(I32).rearrange("a q t -> (a q) t")
+        table = {a: wide_tile([P, T], I32) for a in PASS_ORDER[:-1]}
         w8_raw = wide_tile([P, PACK, M], F32)
-        table = [wide_tile([P, T], I32)]
-        w8_grouped = keep.tile([P, W8_CHUNKS, W8_CHUNK, PACK], BF16, name="w8_grouped", tag="reused", align_bytes=MX_ALIGN)
-        table.extend(wide_tile([P, T], I32) for a in range(1, PASSES))
+        table[PASS_ORDER[-1]] = wide_tile([P, T], I32)
+        w8_grouped = [
+            keep.tile([P, W8_CHUNK, PACK], BF16, name="w8_grouped0", tag="reused", align_bytes=MX_ALIGN),
+            keep.tile([P, W8_CHUNK, PACK], BF16, name="w8_grouped1", align_bytes=MX_ALIGN),
+        ]
         w8_rows = w8.rearrange("(p t) n -> p t n", t=PACK)
 
         def load_words(a, cols):
@@ -91,23 +96,22 @@ def tile_list_tabgate_silu_kernel(
         nc.sync.dma_start(offsets[:], offs)
         nc.sync.dma_start(out=scale_window[32:96:2, :], in_=table_scale_rows[0:32, :])
         nc.sync.dma_start(out=scale_window[33:96:4, :], in_=table_scale_rows[32:48, :])
-        load_words(0, slice(0, T))
+        load_words(PASS_ORDER[0], slice(0, T))
         w4_scale_rows = w4_scales.bitcast(I32).rearrange("a (quad r) n -> r quad a n", r=QUAD_BLOCKS)
         for r in range(QUAD_BLOCKS):
             nc.sync.dma_start(out=w4_planes[r:P:QUAD, :, :], in_=w4_scale_rows[r])
-        nc.sync.dma_start(out=b_rows[0:ROW_TILES, :], in_=b.rearrange("(i p) -> i p", p=P))
+        nc.sync.dma_start(out=b_rows[B_AT : B_AT + ROW_TILES, :], in_=b.rearrange("(i p) -> i p", p=P))
         ident = keep.tile([P, P], F32, name="ident")
         nc.vector.memset(ident[:], 0.0)
         make_identity(nc, ident[:], nomemset=True)
         b_turned = psum.tile([P, BANK], F32, name="acc", tag="acc")
         nc.tensor.transpose(b_turned[:, 0:P], b_rows[:], ident[:])
         bias = keep.tile([P, ROW_TILES], F32, name="bias")
-        nc.scalar.copy(out=bias[:], in_=b_turned[:, 0:ROW_TILES])
+        nc.scalar.copy(out=bias[:], in_=b_turned[:, B_AT : B_AT + ROW_TILES])
+        load_words(PASS_ORDER[1], slice(0, T))
         nc.sync.dma_start(out=w8_raw[:], in_=w8_rows)
-        load_words(1, slice(0, T))
-        load_words(2, slice(0, T))
 
-        picked_words = {a: keep.tile([P, S], U32, name=f"picked{a}", align_bytes=MX_ALIGN) for a in (0, 2)}
+        picked_words = {a: keep.tile([P, S], U32, name=f"picked{a}", align_bytes=MX_ALIGN) for a in PASS_ORDER[:-1]}
         picked_scales = keep.tile([P, S], U8, name="planes0", align_bytes=MX_ALIGN)
         planes = [keep.tile([P, S], U8, name=f"plane{a}", align_bytes=MX_ALIGN) for a in range(PASSES)]
         for plane in planes:
@@ -118,7 +122,7 @@ def tile_list_tabgate_silu_kernel(
             shift = PASS0_SHIFT if a == 0 else 0
             first = WINDOW_AT[a] + WINDOW_STEP[a] * r
             stop = WINDOW_AT[a] + WINDOW_STEP[a] * QUADS * QUAD_BLOCKS
-            queue = nc.sync if a == PASSES - 1 else nc.gpsimd
+            queue = nc.gpsimd if a == 0 else nc.sync
             queue.dma_start(
                 out=planes[a][shift + r : P : QUAD, :].bitcast(I32),
                 in_=picked_scales[first : stop : WINDOW_STEP[a] * QUAD_BLOCKS, :].bitcast(I32),
@@ -131,11 +135,15 @@ def tile_list_tabgate_silu_kernel(
             nc.sync.dma_start(out=gate_tile[:], in_=gT[i * P : (i + 1) * P, :])
             gate_tiles.append(gate_tile)
 
-        moves = [(a, r) for a in range(PASSES) for r in range(QUAD_BLOCKS)]
+        for r in range(QUAD_BLOCKS):
+            move_scale_rows(0, r)
+            move_scale_rows(1, r)
+        load_words(0, slice(0, T))
+        for r in range(QUAD_BLOCKS):
+            move_scale_rows(2, r)
         load_gates(0)
-        for a, r in moves:
-            move_scale_rows(a, r)
-        nc.vector.tensor_copy(picked_words[0][:], table[0][:].bitcast(U32).indirect(offsets[:]))
+        for a in PASS_ORDER[:-1]:
+            nc.vector.tensor_copy(picked_words[a][:], table[a][:].bitcast(U32).indirect(offsets[:]))
 
         w8_codes = keep.tile([P, M], U32, name="w8_codes", align_bytes=MX_ALIGN)
         w8_plane = keep.tile([P, M], U8, name="w8_plane", align_bytes=MX_ALIGN)
@@ -143,22 +151,21 @@ def tile_list_tabgate_silu_kernel(
         def quantise_w8(h):
             features = slice(h * W8_CHUNK, (h + 1) * W8_CHUNK)
             nc.scalar.copy(
-                out=w8_grouped[:, h].rearrange("p (c i) t -> p c t i", i=PACK),
+                out=w8_grouped[h][:].rearrange("p (c i) t -> p c t i", i=PACK),
                 in_=w8_raw[:, :, features].rearrange("p t (c i) -> p c t i", i=PACK),
             )
             nc.vector.quantize_mx(
                 out=w8_codes[:, features].bitcast(FP8X4),
                 scales=w8_plane[:, features],
-                in_=w8_grouped[:, h].rearrange("p n t -> p (n t)"),
+                in_=w8_grouped[h][:].rearrange("p n t -> p (n t)"),
             )
 
         quantise_w8(0)
         quantise_w8(1)
-        picked_words[1] = keep.tile([P, S], U32, name="picked1", tag="reused", align_bytes=MX_ALIGN)
-        nc.vector.tensor_copy(picked_words[1][:], table[1][:].bitcast(U32).indirect(offsets[:]))
+        picked_words[0] = keep.tile([P, S], U32, name="picked0", tag="reused", align_bytes=MX_ALIGN)
 
         for cols in token_slices:
-            nc.vector.tensor_copy(picked_words[PASSES - 1][:, cols], table[-1][:].bitcast(U32).indirect(entries(cols)))
+            nc.vector.tensor_copy(picked_words[0][:, cols], table[0][:].bitcast(U32).indirect(entries(cols)))
 
         for i in range(1, ROW_TILES):
             load_gates(i)
@@ -179,8 +186,8 @@ def tile_list_tabgate_silu_kernel(
                 lhsT_scale=scales,
                 rhs=picked_words[a][:, cols].bitcast(FP8X4),
                 rhs_scale=table_plane,
-                start=(a == 0),
-                stop=(a == PASSES - 1),
+                start=(a == PASS_ORDER[0]),
+                stop=(a == PASS_ORDER[-1]),
             )
 
         def silu_out(act, acc, i, cols):
@@ -189,10 +196,10 @@ def tile_list_tabgate_silu_kernel(
         early = [(i, cols) for cols in token_slices for i in range(EARLY_TILES)]
         early_accs = [psum.tile([P, BANK], F32, name="acc", tag="acc") for unit in early]
         early_acts = [acts.tile([P, S], F32, name="act") for i in range(EARLY_TILES)]
-        for a in range(PASSES):
+        for a in PASS_ORDER:
             for acc, (i, cols) in zip(early_accs, early):
                 mx_pass(acc, a, i, cols)
-                if a == PASSES - 1:
+                if a == PASS_ORDER[-1]:
                     silu_out(early_acts[i], acc, i, cols)
 
         result_all = results.tile([P, ROW_TILES, S], F32, name="result_all", align_bytes=DMA_ALIGN)
@@ -204,7 +211,7 @@ def tile_list_tabgate_silu_kernel(
                 act = acts.tile([P, S], F32, name="act")
                 for cols in token_slices:
                     acc = psum.tile([P, BANK], F32, name="acc", tag="acc")
-                    for a in range(PASSES):
+                    for a in PASS_ORDER:
                         mx_pass(acc, a, i, cols)
                     silu_out(act, acc, i, cols)
 

@@ -34,6 +34,7 @@ DMA_ALIGN = 256
 
 PASS0_SHIFT = 4
 PASS_ORDER = (1, 2, 0)
+SUM_ORDER = (1, 0, 2)
 B_AT = 16
 WINDOW_AT = (32, 64, 33)
 WINDOW_STEP = (2, 2, 4)
@@ -96,9 +97,10 @@ def tile_list_tabgate_silu_kernel(
         nc.sync.dma_start(offsets[:], offs)
         nc.sync.dma_start(out=scale_window[32:96:2, :], in_=table_scale_rows[0:32, :])
         nc.sync.dma_start(out=scale_window[33:96:4, :], in_=table_scale_rows[32:48, :])
-        load_words(PASS_ORDER[0], slice(0, T))
         w4_scale_rows = w4_scales.bitcast(I32).rearrange("a (quad r) n -> r quad a n", r=QUAD_BLOCKS)
-        for r in range(QUAD_BLOCKS):
+        halves = (slice(0, T // 2), slice(T // 2, T))
+        for r, (a, cols) in enumerate((a, cols) for a in PASS_ORDER[:-1] for cols in halves):
+            load_words(a, cols)
             nc.sync.dma_start(out=w4_planes[r:P:QUAD, :, :], in_=w4_scale_rows[r])
         nc.sync.dma_start(out=b_rows[B_AT : B_AT + ROW_TILES, :], in_=b.rearrange("(i p) -> i p", p=P))
         ident = keep.tile([P, P], F32, name="ident")
@@ -108,8 +110,6 @@ def tile_list_tabgate_silu_kernel(
         nc.tensor.transpose(b_turned[:, 0:P], b_rows[:], ident[:])
         bias = keep.tile([P, ROW_TILES], F32, name="bias")
         nc.scalar.copy(out=bias[:], in_=b_turned[:, B_AT : B_AT + ROW_TILES])
-        load_words(PASS_ORDER[1], slice(0, T))
-        nc.sync.dma_start(out=w8_raw[:], in_=w8_rows)
 
         picked_words = {a: keep.tile([P, S], U32, name=f"picked{a}", align_bytes=MX_ALIGN) for a in PASS_ORDER[:-1]}
         picked_scales = keep.tile([P, S], U8, name="planes0", align_bytes=MX_ALIGN)
@@ -122,26 +122,27 @@ def tile_list_tabgate_silu_kernel(
             shift = PASS0_SHIFT if a == 0 else 0
             first = WINDOW_AT[a] + WINDOW_STEP[a] * r
             stop = WINDOW_AT[a] + WINDOW_STEP[a] * QUADS * QUAD_BLOCKS
-            queue = nc.gpsimd if a == 0 else nc.sync
-            queue.dma_start(
+            nc.sync.dma_start(
                 out=planes[a][shift + r : P : QUAD, :].bitcast(I32),
                 in_=picked_scales[first : stop : WINDOW_STEP[a] * QUAD_BLOCKS, :].bitcast(I32),
             )
 
         gate_tiles = []
 
-        def load_gates(i):
-            gate_tile = wide_tile([P, T], F32)
-            nc.sync.dma_start(out=gate_tile[:], in_=gT[i * P : (i + 1) * P, :])
-            gate_tiles.append(gate_tile)
+        def load_gates(i, cols=slice(0, T)):
+            if cols.start == 0:
+                gate_tiles.append(wide_tile([P, T], F32))
+            nc.sync.dma_start(out=gate_tiles[i][:, cols], in_=gT[i * P : (i + 1) * P, cols])
 
-        for r in range(QUAD_BLOCKS):
-            move_scale_rows(0, r)
-            move_scale_rows(1, r)
-        load_words(0, slice(0, T))
-        for r in range(QUAD_BLOCKS):
-            move_scale_rows(2, r)
-        load_gates(0)
+        half_loads = [lambda t=t: nc.sync.dma_start(out=w8_raw[:, t : t + 2], in_=w8_rows[:, t : t + 2]) for t in (0, 2)]
+        half_loads += [lambda cols=cols: load_words(0, cols) for cols in halves]
+        half_loads += [lambda i=i, cols=cols: load_gates(i, cols) for i in range(2) for cols in halves]
+        for step, half_load in enumerate(half_loads):
+            half_load()
+            a, r = divmod(step, QUAD_BLOCKS)
+            move_scale_rows(1 + a, r)
+            if a == 0:
+                move_scale_rows(0, r)
         for a in PASS_ORDER[:-1]:
             nc.vector.tensor_copy(picked_words[a][:], table[a][:].bitcast(U32).indirect(offsets[:]))
 
@@ -167,7 +168,7 @@ def tile_list_tabgate_silu_kernel(
         for cols in token_slices:
             nc.vector.tensor_copy(picked_words[0][:, cols], table[0][:].bitcast(U32).indirect(entries(cols)))
 
-        for i in range(1, ROW_TILES):
+        for i in range(len(gate_tiles), ROW_TILES):
             load_gates(i)
 
         def mx_pass(acc, a, i, cols):
@@ -186,8 +187,8 @@ def tile_list_tabgate_silu_kernel(
                 lhsT_scale=scales,
                 rhs=picked_words[a][:, cols].bitcast(FP8X4),
                 rhs_scale=table_plane,
-                start=(a == PASS_ORDER[0]),
-                stop=(a == PASS_ORDER[-1]),
+                start=(a == SUM_ORDER[0]),
+                stop=(a == SUM_ORDER[-1]),
             )
 
         def silu_out(act, acc, i, cols):
@@ -196,10 +197,10 @@ def tile_list_tabgate_silu_kernel(
         early = [(i, cols) for cols in token_slices for i in range(EARLY_TILES)]
         early_accs = [psum.tile([P, BANK], F32, name="acc", tag="acc") for unit in early]
         early_acts = [acts.tile([P, S], F32, name="act") for i in range(EARLY_TILES)]
-        for a in PASS_ORDER:
+        for a in SUM_ORDER:
             for acc, (i, cols) in zip(early_accs, early):
                 mx_pass(acc, a, i, cols)
-                if a == PASS_ORDER[-1]:
+                if a == SUM_ORDER[-1]:
                     silu_out(early_acts[i], acc, i, cols)
 
         result_all = results.tile([P, ROW_TILES, S], F32, name="result_all", align_bytes=DMA_ALIGN)
@@ -211,7 +212,7 @@ def tile_list_tabgate_silu_kernel(
                 act = acts.tile([P, S], F32, name="act")
                 for cols in token_slices:
                     acc = psum.tile([P, BANK], F32, name="acc", tag="acc")
-                    for a in PASS_ORDER:
+                    for a in SUM_ORDER:
                         mx_pass(acc, a, i, cols)
                     silu_out(act, acc, i, cols)
 

@@ -194,7 +194,7 @@ def tile_list_tabgate_silu_kernel(
         def silu_out(act, acc, i, cols):
             nc.scalar.activation(out=act[:, cols], in_=acc[:], func=SILU, bias=bias[:, i : i + 1])
 
-        early = [(i, cols) for cols in token_slices for i in range(EARLY_TILES)]
+        early = [(i, cols) for i in range(EARLY_TILES) for cols in token_slices]
         early_accs = [psum.tile([P, BANK], F32, name="acc", tag="acc") for unit in early]
         early_acts = [acts.tile([P, S], F32, name="act") for i in range(EARLY_TILES)]
         for a in SUM_ORDER:
@@ -210,11 +210,12 @@ def tile_list_tabgate_silu_kernel(
                 act = early_acts[i]
             else:
                 act = acts.tile([P, S], F32, name="act")
-                for cols in token_slices:
-                    acc = psum.tile([P, BANK], F32, name="acc", tag="acc")
-                    for a in SUM_ORDER:
+                accs = [psum.tile([P, BANK], F32, name="acc", tag="acc") for cols in token_slices]
+                for a in SUM_ORDER:
+                    for acc, cols in zip(accs, token_slices):
                         mx_pass(acc, a, i, cols)
-                    silu_out(act, acc, i, cols)
+                        if a == SUM_ORDER[-1]:
+                            silu_out(act, acc, i, cols)
 
             result = result_all[:, i, :]
             if i == ROW_TILES - 1:

@@ -136,13 +136,13 @@ def tile_list_tabgate_silu_kernel(
 
         half_loads = [lambda t=t: nc.sync.dma_start(out=w8_raw[:, t : t + 2], in_=w8_rows[:, t : t + 2]) for t in (0, 2)]
         half_loads += [lambda cols=cols: load_words(0, cols) for cols in halves]
-        half_loads += [lambda i=i, cols=cols: load_gates(i, cols) for i in range(2) for cols in halves]
+        half_loads += [lambda cols=cols: load_gates(0, cols) for cols in halves]
+        moves = [(a, r) for r in range(QUAD_BLOCKS) for a in SUM_ORDER[:-1]]
+        moves += [(SUM_ORDER[-1], r) for r in range(QUAD_BLOCKS)]
         for step, half_load in enumerate(half_loads):
             half_load()
-            a, r = divmod(step, QUAD_BLOCKS)
-            move_scale_rows(1 + a, r)
-            if a == 0:
-                move_scale_rows(0, r)
+            for a, r in moves[2 * step : 2 * step + 2]:
+                move_scale_rows(a, r)
         for a in PASS_ORDER[:-1]:
             nc.vector.tensor_copy(picked_words[a][:], table[a][:].bitcast(U32).indirect(offsets[:]))
 

@@ -45,7 +45,7 @@ PSUM_BANKS = 8
 W8_CHUNKS = 2
 EARLY_TILES = PSUM_BANKS * BANK // S
 W8_CHUNK = M // W8_CHUNKS
-STORE_FROM = {4: 0, 6: 4, 7: 6}
+STORE_FROM = {i + 1: i for i in range(ROW_TILES - 1)}
 LAST_TILE_PIECES = ((0, 1024), (1024, 1792), (1792, 2048))
 
 

from contextlib import ExitStack

import concourse.mybir as mybir
from concourse.masks import make_identity

K, M, T, S = 1536, 1024, 4096, 2048
FLOPS = 2 * K * M * S

F32 = mybir.dt.float32
BF16 = mybir.dt.bfloat16
I32 = mybir.dt.int32
U32 = mybir.dt.uint32
U16 = mybir.dt.uint16
U8 = mybir.dt.uint8
FP8X4 = mybir.dt.float8_e4m3fn_x4
FP4X4 = mybir.dt.float4_e2m1fn_x4
SILU = mybir.ActivationFunctionType.Silu
MULT = mybir.AluOpType.mult

P = 128
PACK = 4
PASSES = K // (P * PACK)
W4_PASSES = PASSES - 1
W4_WORD_BYTES = 2
BYTES_PER_I32 = 4
BANK = 512
STRIPE = 16
ROW_TILES = M // P
QUADS = 4
QUAD = P // QUADS
QUAD_BLOCKS = 4
MX_ALIGN = 64
DMA_ALIGN = 256

PASS0_SHIFT = 4
PASS_ORDER = (1, 2, 0)
SUM_ORDER = (1, 0, 2)
B_AT = 16
WINDOW_AT = (32, 64, 33)
WINDOW_STEP = (2, 2, 4)

WIDE_SLOTS = 6
ACT_SLOTS = 3
PSUM_BANKS = 8
W8_CHUNKS = 2
EARLY_TILES = PSUM_BANKS * BANK // S
W8_CHUNK = M // W8_CHUNKS
STORE_FROM = {i + 1: i for i in range(ROW_TILES - 1)}
LAST_TILE_PIECES = ((0, 1024), (1024, 1792), (1792, 2048))


def tile_list_tabgate_silu_kernel(
    tc, tab_words, tab_scales, w8, w4_words, w4_scales, gT, b, offs, out
):
    nc = tc.nc
    token_slices = [slice(j, j + BANK) for j in range(0, S, BANK)]
    with ExitStack() as ctx:
        keep = ctx.enter_context(tc.tile_pool(name="keep", bufs=1))
        wide = ctx.enter_context(tc.tile_pool(name="wide", bufs=WIDE_SLOTS))
        results = ctx.enter_context(tc.tile_pool(name="results", bufs=1))
        acts = ctx.enter_context(tc.tile_pool(name="acts", bufs=ACT_SLOTS))
        psum = ctx.enter_context(tc.psum_pool(name="psum", bufs=PSUM_BANKS))

        def wide_tile(shape, dtype):
            return wide.tile(shape, dtype, name="wide_tile", tag="wide", align_bytes=DMA_ALIGN)

        scale_window = wide_tile([P, T // BYTES_PER_I32], I32)
        nc.vector.memset(scale_window[:], 0)
        offsets = keep.tile([P, S // STRIPE], U16, name="offsets")

        def entries(cols):
            return offsets[:, cols.start // STRIPE : cols.stop // STRIPE]

        w4_planes = keep.tile([P, W4_PASSES, M // BYTES_PER_I32], I32, name="w4_planes", align_bytes=MX_ALIGN)
        nc.vector.memset(w4_planes[:], 0)
        b_rows = keep.tile([P, P], F32, name="b_rows")
        nc.vector.memset(b_rows[:], 0.0)

        table_scale_rows = tab_scales.bitcast(I32).rearrange("a q t -> (a q) t")
        table = {a: wide_tile([P, T], I32) for a in PASS_ORDER[:-1]}
        w8_raw = wide_tile([P, PACK, M], F32)
        table[PASS_ORDER[-1]] = wide_tile([P, T], I32)
        w8_grouped = [
            keep.tile([P, W8_CHUNK, PACK], BF16, name="w8_grouped0", tag="reused", align_bytes=MX_ALIGN),
            keep.tile([P, W8_CHUNK, PACK], BF16, name="w8_grouped1", align_bytes=MX_ALIGN),
        ]
        w8_rows = w8.rearrange("(p t) n -> p t n", t=PACK)

        def load_words(a, cols):
            words = tab_words[a].rearrange("p t i -> p (t i)").bitcast(I32)
            nc.sync.dma_start(out=table[a][:, cols], in_=words[:, cols])

        w4_codes = keep.tile(
            [P, W4_PASSES, W4_WORD_BYTES * M // BYTES_PER_I32], I32, name="w4_codes", align_bytes=DMA_ALIGN
        )
        nc.sync.dma_start(out=w4_codes[:], in_=w4_words.bitcast(I32).rearrange("a p n -> p a n"))
        nc.sync.dma_start(offsets[:], offs)
        nc.sync.dma_start(out=scale_window[32:96:2, :], in_=table_scale_rows[0:32, :])
        nc.sync.dma_start(out=scale_window[33:96:4, :], in_=table_scale_rows[32:48, :])
        w4_scale_rows = w4_scales.bitcast(I32).rearrange("a (quad r) n -> r quad a n", r=QUAD_BLOCKS)
        halves = (slice(0, T // 2), slice(T // 2, T))
        for r, (a, cols) in enumerate((a, cols) for a in PASS_ORDER[:-1] for cols in halves):
            load_words(a, cols)
            nc.sync.dma_start(out=w4_planes[r:P:QUAD, :, :], in_=w4_scale_rows[r])
        nc.sync.dma_start(out=b_rows[B_AT : B_AT + ROW_TILES, :], in_=b.rearrange("(i p) -> i p", p=P))
        ident = keep.tile([P, P], F32, name="ident")
        nc.vector.memset(ident[:], 0.0)
        make_identity(nc, ident[:], nomemset=True)
        b_turned = psum.tile([P, BANK], F32, name="acc", tag="acc")
        nc.tensor.transpose(b_turned[:, 0:P], b_rows[:], ident[:])
        bias = keep.tile([P, ROW_TILES], F32, name="bias")
        nc.scalar.copy(out=bias[:], in_=b_turned[:, B_AT : B_AT + ROW_TILES])

        picked_words = {a: keep.tile([P, S], U32, name=f"picked{a}", align_bytes=MX_ALIGN) for a in PASS_ORDER[:-1]}
        picked_scales = keep.tile([P, S], U8, name="planes0", align_bytes=MX_ALIGN)
        planes = [keep.tile([P, S], U8, name=f"plane{a}", align_bytes=MX_ALIGN) for a in range(PASSES)]
        for plane in planes:
            nc.vector.memset(plane[:].bitcast(I32), 0)
        nc.vector.tensor_copy(picked_scales[:], scale_window[:].bitcast(U8).indirect(offsets[:]))

        def move_scale_rows(a, r):
            shift = PASS0_SHIFT if a == 0 else 0
            first = WINDOW_AT[a] + WINDOW_STEP[a] * r
            stop = WINDOW_AT[a] + WINDOW_STEP[a] * QUADS * QUAD_BLOCKS
            nc.sync.dma_start(
                out=planes[a][shift + r : P : QUAD, :].bitcast(I32),
                in_=picked_scales[first : stop : WINDOW_STEP[a] * QUAD_BLOCKS, :].bitcast(I32),
            )

        gate_tiles = []

        def load_gates(i, cols=slice(0, T)):
            if cols.start == 0:
                gate_tiles.append(wide_tile([P, T], F32))
            nc.sync.dma_start(out=gate_tiles[i][:, cols], in_=gT[i * P : (i + 1) * P, cols])

        half_loads = [lambda t=t: nc.sync.dma_start(out=w8_raw[:, t : t + 2], in_=w8_rows[:, t : t + 2]) for t in (0, 2)]
        half_loads += [lambda cols=cols: load_words(0, cols) for cols in halves]
        half_loads += [lambda cols=cols: load_gates(0, cols) for cols in halves]
        moves = [(a, r) for r in range(QUAD_BLOCKS) for a in SUM_ORDER[:-1]]
        moves += [(SUM_ORDER[-1], r) for r in range(QUAD_BLOCKS)]
        for step, half_load in enumerate(half_loads):
            half_load()
            for a, r in moves[2 * step : 2 * step + 2]:
                move_scale_rows(a, r)
        for a in PASS_ORDER[:-1]:
            nc.vector.tensor_copy(picked_words[a][:], table[a][:].bitcast(U32).indirect(offsets[:]))

        w8_codes = keep.tile([P, M], U32, name="w8_codes", align_bytes=MX_ALIGN)
        w8_plane = keep.tile([P, M], U8, name="w8_plane", align_bytes=MX_ALIGN)

        def quantise_w8(h):
            features = slice(h * W8_CHUNK, (h + 1) * W8_CHUNK)
            nc.scalar.copy(
                out=w8_grouped[h][:].rearrange("p (c i) t -> p c t i", i=PACK),
                in_=w8_raw[:, :, features].rearrange("p t (c i) -> p c t i", i=PACK),
            )
            nc.vector.quantize_mx(
                out=w8_codes[:, features].bitcast(FP8X4),
                scales=w8_plane[:, features],
                in_=w8_grouped[h][:].rearrange("p n t -> p (n t)"),
            )

        quantise_w8(0)
        quantise_w8(1)
        picked_words[0] = keep.tile([P, S], U32, name="picked0", tag="reused", align_bytes=MX_ALIGN)

        for cols in token_slices:
            nc.vector.tensor_copy(picked_words[0][:, cols], table[0][:].bitcast(U32).indirect(entries(cols)))

        for i in range(len(gate_tiles), ROW_TILES):
            load_gates(i)

        def mx_pass(acc, a, i, cols):
            rows = slice(i * P, (i + 1) * P)
            if a == 0:
                codes, scales = w8_codes[:, rows].bitcast(FP8X4), w8_plane[:, rows]
                table_plane = planes[0][PASS0_SHIFT:P, cols]
            else:
                w4_bytes = slice(W4_WORD_BYTES * rows.start, W4_WORD_BYTES * rows.stop)
                codes = w4_codes[:, a - 1, :].bitcast(U8)[:, w4_bytes].bitcast(FP4X4)
                scales = w4_planes[:, a - 1, :].bitcast(U8)[:, rows]
                table_plane = planes[a][:, cols]
            nc.tensor.matmul_mx(
                out=acc[:],
                lhsT=codes,
                lhsT_scale=scales,
                rhs=picked_words[a][:, cols].bitcast(FP8X4),
                rhs_scale=table_plane,
                start=(a == SUM_ORDER[0]),
                stop=(a == SUM_ORDER[-1]),
            )

        def silu_out(act, acc, i, cols):
            nc.scalar.activation(out=act[:, cols], in_=acc[:], func=SILU, bias=bias[:, i : i + 1])

        early = [(i, cols) for i in range(EARLY_TILES) for cols in token_slices]
        early_accs = [psum.tile([P, BANK], F32, name="acc", tag="acc") for unit in early]
        early_acts = [acts.tile([P, S], F32, name="act") for i in range(EARLY_TILES)]
        for a in SUM_ORDER:
            for acc, (i, cols) in zip(early_accs, early):
                mx_pass(acc, a, i, cols)
                if a == SUM_ORDER[-1]:
                    silu_out(early_acts[i], acc, i, cols)

        result_all = results.tile([P, ROW_TILES, S], F32, name="result_all", align_bytes=DMA_ALIGN)
        for i in range(ROW_TILES):
            gates = gate_tiles[i]
            if i < EARLY_TILES:
                act = early_acts[i]
            else:
                act = acts.tile([P, S], F32, name="act")
                accs = [psum.tile([P, BANK], F32, name="acc", tag="acc") for cols in token_slices]
                for a in SUM_ORDER:
                    for acc, cols in zip(accs, token_slices):
                        mx_pass(acc, a, i, cols)
                        if a == SUM_ORDER[-1]:
                            silu_out(act, acc, i, cols)

            result = result_all[:, i, :]
            if i == ROW_TILES - 1:
                for first, last in LAST_TILE_PIECES:
                    cols = slice(first, last)
                    nc.vector.tensor_tensor(result[:, cols], gates[:].indirect(entries(cols)), act[:, cols], MULT)
                    nc.sync.dma_start(out=out[i * P : (i + 1) * P, cols], in_=result[:, cols])
            elif i == 0:
                for cols in token_slices:
                    nc.vector.tensor_tensor(result[:, cols], gates[:].indirect(entries(cols)), act[:, cols], MULT)
            else:
                nc.vector.tensor_tensor(result, gates[:].indirect(offsets[:]), act[:], MULT)
            if i + 1 in STORE_FROM:
                first = STORE_FROM[i + 1]
                stored_rows = out[first * P : (i + 1) * P, :].rearrange("(h p) j -> p h j", p=P)
                nc.sync.dma_start(out=stored_rows, in_=result_all[:, first : i + 1, :])
